import numpy as np
import ml_dtypes


def mxq(x, axis, fmt="e4m3"):
    dtype, down = {"e4m3": (ml_dtypes.float8_e4m3fn, 7), "e5m2": (ml_dtypes.float8_e5m2, 14)}[fmt]
    v = np.moveaxis(np.asarray(x, np.float32).astype(ml_dtypes.bfloat16).astype(np.float64), axis, -1)
    blocks = v.reshape(v.shape[:-1] + (-1, 32))
    amax = np.abs(blocks).max(-1, keepdims=True)
    byte = np.maximum(np.where(amax > 0, np.frexp(amax)[1] - 1 + 127, 0) - down, 1)
    scale = np.exp2(byte - 127.0)
    codes = (blocks / scale).astype(np.float32).astype(dtype).astype(np.float64)
    return np.moveaxis((codes * scale).reshape(v.shape), -1, axis)


WIDE = False


def mx_kscale(k):
    if not WIDE:
        return np.ones(k)
    levels = np.array([10, -10, 5, -5, 0])
    if k % 512:
        return np.exp2(np.random.permutation(np.resize(levels, k // 32))).repeat(32)
    a = np.empty((k // 512, 16))
    for p in range(k // 512):
        a[p, :8] = np.random.permutation(np.resize(levels, 8))
        for g in range(8):
            far = levels[np.abs(levels - a[p, g]) >= 10]
            a[p, g + 8] = far[np.random.randint(len(far))]
    return np.exp2(a.ravel()).repeat(32)


def f64(x):
    return np.asarray(x).astype(np.float64)


def striped(idx):
    return np.tile(idx.reshape(-1, 16).T, (8, 1)).astype(np.uint16)


def unstriped(offs):
    return offs[:16].T.reshape(-1).astype(np.int64)


E2M1 = np.array([0.0, 0.5, 1.0, 1.5, 2.0, 3.0, 4.0, 6.0, -0.0, -0.5, -1.0, -1.5, -2.0, -3.0, -4.0, -6.0])


def pack_weight(w, fmt):
    k, n = w.shape
    w = f64(np.asarray(w, np.float32).astype(ml_dtypes.bfloat16)).reshape(k // 32, 32, n)
    amax = np.abs(w).max(1)
    if fmt == "e4m3":
        byte = np.frexp(amax)[1] - 1 + 127 - 7
    else:
        mant, ex = np.frexp(amax / 6.0)
        byte = np.where(mant > 0.5, ex, ex - 1) + 127
    byte = np.clip(np.where(amax > 0, byte, 1), 1, 254)
    scaled = (w * np.exp2(127.0 - byte)[:, None, :]).reshape(k, n).astype(np.float32)
    by_word = np.ascontiguousarray(scaled.reshape(k // 512, 128, 4, n).transpose(0, 1, 3, 2))
    if fmt == "e4m3":
        words = by_word.astype(ml_dtypes.float8_e4m3fn).view(np.uint8)
    else:
        c = by_word.astype(ml_dtypes.float4_e2m1fn).view(np.uint8) & 0xF
        words = (c[..., 0::2] | (c[..., 1::2] << 4)).reshape(k // 512, 128, 2 * n)
    return np.ascontiguousarray(words), np.ascontiguousarray(byte.astype(np.uint8).reshape(k // 512, 16, n))


def unpack_weight(words, scales, fmt):
    g, _, n = scales.shape
    words = np.ascontiguousarray(words).reshape(g, 128, n, -1)
    if fmt == "e4m3":
        vals = words.view(ml_dtypes.float8_e4m3fn).astype(np.float64)
    else:
        nib = np.empty((g, 128, n, 4), np.uint8)
        nib[..., 0::2] = words & 0xF
        nib[..., 1::2] = words >> 4
        vals = E2M1[nib]
    vals = vals * np.repeat(np.exp2(scales.astype(np.float64) - 127.0), 8, axis=1)[..., None]
    return vals.transpose(0, 1, 3, 2).reshape(g * 512, n)


def silu(v):
    return v / (1.0 + np.exp(-np.maximum(v, -700.0)))


K, T, E, C, H, N = 512, 512, 4, 256, 1024, 512


def by_expert(wq, xq):
    return np.concatenate([wq[e].T @ xq[:, e * C:(e + 1) * C] for e in range(E)], axis=1)


def setup_inputs():
    n = np.random.standard_normal
    s = mx_kscale(K)[:, None]
    u = mx_kscale(H)
    first = np.random.permutation(np.repeat(np.arange(E), T // E))
    second = (first + 1 + np.random.permutation(np.repeat(np.arange(E - 1), -(-T // (E - 1)))[:T])) % E
    while np.bincount(second, minlength=E).max() != T // E:
        load = np.bincount(second, minlength=E); hi, lo = int(load.argmax()), int(load.argmin())
        t = np.flatnonzero((second == hi) & (first != lo))[0]; second[t] = lo
    slot_token = np.empty(E * C, np.int64); pos = np.empty((2, T), np.int64); fill = np.zeros(E, np.int64)
    place = np.stack([np.random.permutation(C) for _ in range(E)])
    for r, deal in enumerate((first, second)):
        for t in np.random.permutation(T):
            e = deal[t]; j = e * C + place[e, fill[e]]; fill[e] += 1; slot_token[j] = t; pos[r, t] = j
    g = np.random.uniform(0.2, 0.8, T)
    w1 = [pack_weight(m, "e2m1") for m in n((E, K, H)) / np.sqrt(K) / s[None] * u[None, None, :]]
    w2 = [pack_weight(m, "e2m1") for m in n((E, H, N)) / np.sqrt(H) / u[None, :, None]]
    x = pack_weight(n((K, T)) * s, "e4m3")
    return {
        "x_words": x[0],
        "x_scales": x[1],
        "w1_words": np.stack([m[0] for m in w1]),
        "w1_scales": np.stack([m[1] for m in w1]),
        "w2_words": np.stack([m[0] for m in w2]),
        "w2_scales": np.stack([m[1] for m in w2]),
        "gate": np.stack([np.tile(g, (N, 1)), np.tile(1.0 - g, (N, 1))]).astype(np.float32),
        "offs": striped(slot_token),
        "pos1": striped(pos[0]),
        "pos2": striped(pos[1]),
    }


def reference(x_words, x_scales, w1_words, w1_scales, w2_words, w2_scales, gate, offs, pos1, pos2):
    idx = unstriped(offs)
    w1 = np.stack([unpack_weight(w1_words[e], w1_scales[e], "e2m1") for e in range(E)])
    w2 = np.stack([unpack_weight(w2_words[e], w2_scales[e], "e2m1") for e in range(E)])
    xq = unpack_weight(x_words, x_scales, "e4m3")[:, idx]
    h = silu(by_expert(w1, xq))
    y = by_expert(w2, mxq(h, 0, "e4m3"))
    return f64(gate[0]) * y[:, unstriped(pos1)] + f64(gate[1]) * y[:, unstriped(pos2)]

@@ -1,0 +1,246 @@
+from contextlib import ExitStack
+
+import concourse.mybir as mybir
+
+K, T, E, C, H, N = 512, 512, 4, 256, 1024, 512
+SLOTS = E * C
+P = 128
+PACK = 4
+K_PASS = P * PACK
+H_PASSES = H // K_PASS
+N_TILES = N // P
+CHUNK = 128
+CHUNKS = SLOTS // CHUNK
+GROUP = 16
+
+F32 = mybir.dt.float32
+BF16 = mybir.dt.bfloat16
+I32 = mybir.dt.int32
+U32 = mybir.dt.uint32
+U16 = mybir.dt.uint16
+U8 = mybir.dt.uint8
+FP8X4 = mybir.dt.float8_e4m3fn_x4
+FP4X4 = mybir.dt.float4_e2m1fn_x4
+SILU = mybir.ActivationFunctionType.Silu
+MULT = mybir.AluOpType.mult
+ADD = mybir.AluOpType.add
+
+FLOPS = 2 * SLOTS * (K * H + H * N)
+
+
+def tile_moe_pkd_mlp_silu_kernel(
+    tc, x_words, x_scales, w1_words, w1_scales, w2_words, w2_scales, gate, offs, pos1, pos2, out
+):
+    nc = tc.nc
+    with ExitStack() as ctx:
+        keep = ctx.enter_context(tc.tile_pool(name="keep", bufs=1))
+        ring = ctx.enter_context(tc.tile_pool(name="ring", bufs=4))
+        pair = ctx.enter_context(tc.tile_pool(name="pair", bufs=4))
+        psum = ctx.enter_context(tc.psum_pool(name="psum", bufs=8))
+
+        offs_sb = keep.tile([P, SLOTS // GROUP], U16, name="offs_sb")
+        pos1_sb = keep.tile([P, T // GROUP], U16, name="pos1_sb")
+        pos2_sb = keep.tile([P, T // GROUP], U16, name="pos2_sb")
+        xw = keep.tile([P, T], I32, name="xw", align_bytes=64)
+        xs = keep.tile([P, T], U8, name="xs", align_bytes=64)
+        w1_raw = [keep.tile([P, 2 * H], U8, name="w1_raw%d" % e, tag="w1_raw%d" % e, align_bytes=64) for e in range(E)]
+        w1s_pair = [keep.tile([P, 2, H], U8, name="w1s_pair%d" % i, align_bytes=64) for i in range(E // 2)]
+        w1s_raw = [w1s_pair[e // 2][:, e % 2, :] for e in range(E)]
+        w1sp = [keep.tile([P, H], U8, name="w1sp%d" % e, align_bytes=64) for e in range(E)]
+        w2w = [keep.tile([P, H_PASSES, 2 * N], U8, name="w2w%d" % e, align_bytes=64) for e in range(E)]
+        w2s = keep.tile([P, E * H_PASSES, N], U8, name="w2s", align_bytes=64)
+        gates = [keep.tile([P, 2, T], F32, name="gates%d" % j) for j in range(N_TILES)]
+        hs = keep.tile([P, CHUNKS, H_PASSES, CHUNK], U8, name="hs", align_bytes=64)
+        y = [keep.tile([P, SLOTS], F32, name="y%d" % j) for j in range(N_TILES)]
+        warm = keep.tile([P, 2], F32, name="warm")
+
+        nc.gpsimd.memset(xs[:].bitcast(I32), 0)
+        nc.gpsimd.memset(w1s_pair[0][:].rearrange("p e i -> p (e i)").bitcast(I32), 0)
+        nc.gpsimd.memset(warm[:, 0:1], 0.0)
+        nc.gpsimd.memset(w1s_pair[1][:].rearrange("p e i -> p (e i)").bitcast(I32), 0)
+        nc.gpsimd.memset(w2s[:].rearrange("p a n -> p (a n)").bitcast(I32), 0)
+
+        xs_rows = x_scales[0].rearrange("(q r) t -> r q t", r=4)
+        w1s_rows = w1_scales.rearrange("e s (q r) i -> r q (e s) i", r=4)
+        w2s_rows = w2_scales.rearrange("e s (q r) n -> r q (e s) n", r=4)
+
+        nc.sync.dma_start(offs_sb[:], offs)
+        nc.sync.dma_start(w1_raw[0][:, 0:H].bitcast(I32), w1_words[0, 0, :, 0:H].bitcast(I32))
+        nc.sync.dma_start(xw[:], x_words[0].rearrange("p t r -> p (t r)").bitcast(I32))
+        for r in range(4):
+            nc.scalar.dma_start(xs[r:P:32, :].bitcast(I32), xs_rows[r].bitcast(I32))
+        for r in range(4):
+            queue = nc.scalar if r == 0 else nc.sync
+            queue.dma_start(w1s_pair[0][r:P:32, :, :].bitcast(I32), w1s_rows[r, :, 0:2, :].bitcast(I32))
+        nc.sync.dma_start(w1_raw[0][:, H : 2 * H].bitcast(I32), w1_words[0, 0, :, H : 2 * H].bitcast(I32))
+        nc.sync.dma_start(w1_raw[1][:].bitcast(I32), w1_words[1, 0].bitcast(I32))
+        nc.sync.dma_start(w1_raw[2][:].bitcast(I32), w1_words[2, 0].bitcast(I32))
+        for r in range(4):
+            queue = nc.scalar if r < 2 else nc.sync
+            queue.dma_start(w1s_pair[1][r:P:32, :, :].bitcast(I32), w1s_rows[r, :, 2:4, :].bitcast(I32))
+        nc.scalar.activation(out=warm[:, 1:2], in_=warm[:, 0:1], func=SILU)
+        nc.sync.dma_start(w1_raw[3][:].bitcast(I32), w1_words[3, 0].bitcast(I32))
+        for r in range(4):
+            nc.sync.dma_start(w2s[r:P:32, :, :].bitcast(I32), w2s_rows[r].bitcast(I32))
+        for e in range(E):
+            nc.sync.dma_start(w2w[e][:].bitcast(I32), w2_words[e].rearrange("s p b -> p s b").bitcast(I32))
+        nc.sync.dma_start(pos1_sb[:], pos1)
+        nc.sync.dma_start(pos2_sb[:], pos2)
+        for j in range(N_TILES):
+            nc.sync.dma_start(gates[j][:], gate[:, j * P : (j + 1) * P, :].rearrange("g p t -> p g t"))
+
+        xg, xsg, w1p = {}, {}, {}
+
+        def gather_tokens(c):
+            entries = offs_sb[:, c * CHUNK // GROUP : (c + 1) * CHUNK // GROUP]
+            xg[c] = pair.tile([P, CHUNK], U32, name="xg", align_bytes=64)
+            xsg[c] = pair.tile([P, CHUNK], U8, name="xsg", align_bytes=64)
+            nc.vector.tensor_copy(xg[c][:], xw[:].bitcast(U32).indirect(entries))
+            nc.vector.tensor_copy(xsg[c][:], xs[:].indirect(entries))
+
+        def permute_w1(e, s):
+            cols = slice(s * K_PASS, (s + 1) * K_PASS)
+            w1p[(e, s)] = keep.tile([P, 2 * K_PASS], U8, name="w1p%d_%d" % (e, s), align_bytes=64)
+            nc.vector.tensor_copy(
+                out=w1p[(e, s)][:].bitcast(U16).rearrange("p (t m) -> p t m", t=PACK),
+                in_=w1_raw[e][:].bitcast(U16)[:, cols].rearrange("p (m t) -> p t m", t=PACK),
+            )
+
+        def permute_w1_scales(e, s):
+            cols = slice(s * K_PASS, (s + 1) * K_PASS)
+            nc.vector.tensor_copy(
+                out=w1sp[e][:, cols].rearrange("p (t m) -> p t m", t=PACK),
+                in_=w1s_raw[e][:, cols].rearrange("p (m t) -> p t m", t=PACK),
+            )
+
+        h_bf = {}
+
+        def first_layer(c, s):
+            e = c * CHUNK // C
+            if c not in h_bf:
+                h_bf[c] = keep.tile([P, H_PASSES, CHUNK, PACK], BF16, name="h_bf%d" % c, align_bytes=64)
+            a = psum.tile([P, PACK, CHUNK], F32, name="a", tag="bank")
+            for t in range(PACK):
+                col = s * K_PASS + t * P
+                nc.tensor.matmul_mx(
+                    out=a[:, t, :],
+                    lhsT=w1p[(e, s)][:, 2 * t * P : 2 * (t + 1) * P].bitcast(FP4X4),
+                    lhsT_scale=w1sp[e][:, col : col + P],
+                    rhs=xg[c][:].bitcast(FP8X4),
+                    rhs_scale=xsg[c][:],
+                    start=True,
+                    stop=True,
+                )
+            nc.scalar.activation(out=h_bf[c][:, s, :, :], in_=a[:].rearrange("p t c -> p c t"), func=SILU)
+
+        def quantize(c):
+            nc.vector.quantize_mx(
+                out=hq[:, c, :, :].rearrange("p s c -> p (s c)").bitcast(FP8X4),
+                scales=hs[:, c, :, :].rearrange("p s c -> p (s c)"),
+                in_=h_bf[c][:].rearrange("p s c t -> p (s c t)"),
+            )
+
+        banks = {}
+
+        def second_layer(j, c, first):
+            e = c * CHUNK // C
+            if (j, first) not in banks:
+                banks[(j, first)] = psum.tile([P, 4, CHUNK], F32, name="yb", tag="bank")
+            for s in range(H_PASSES):
+                nc.tensor.matmul_mx(
+                    out=banks[(j, first)][:, c - first, :],
+                    lhsT=w2w[e][:, s, 2 * j * P : 2 * (j + 1) * P].bitcast(FP4X4),
+                    lhsT_scale=w2s[:, e * H_PASSES + s, j * P : (j + 1) * P],
+                    rhs=hq[:, c, s, :].bitcast(FP8X4),
+                    rhs_scale=hs[:, c, s, :],
+                    start=(s == 0),
+                    stop=(s == H_PASSES - 1),
+                )
+
+        def evacuate(j, first, last):
+            nc.scalar.copy(
+                out=y[j][:, first * CHUNK : last * CHUNK],
+                in_=banks[(j, first)][:, 0 : last - first, :].rearrange("p a c -> p (a c)"),
+            )
+
+        picked = {}
+
+        def pick(j, g, first, count):
+            tokens = slice(first, first + count)
+            pos = (pos1_sb, pos2_sb)[g]
+            if j not in picked:
+                picked[j] = ring.tile([P, 2, T], F32, name="picked")
+            nc.vector.tensor_tensor(
+                picked[j][:, g, tokens],
+                y[j][:].indirect(pos[:, first // GROUP : (first + count) // GROUP]),
+                gates[j][:, g, tokens],
+                MULT,
+            )
+
+        results = {}
+
+        def combine(j, first, count):
+            tokens = slice(first, first + count)
+            if j not in results:
+                results[j] = ring.tile([P, T], F32, name="result")
+            nc.vector.tensor_tensor(results[j][:, tokens], picked[j][:, 0, tokens], picked[j][:, 1, tokens], ADD)
+            nc.sync.dma_start(out[j * P : (j + 1) * P, tokens], results[j][:, tokens])
+
+        permute_w1(0, 0)
+        gather_tokens(0)
+        gather_tokens(1)
+        permute_w1_scales(0, 0)
+        first_layer(0, 0)
+        first_layer(1, 0)
+        permute_w1(0, 1)
+        permute_w1_scales(0, 1)
+        first_layer(0, 1)
+        first_layer(1, 1)
+        for e in range(1, E):
+            gather_tokens(2 * e)
+            permute_w1(e, 0)
+            permute_w1_scales(e, 0)
+            first_layer(2 * e, 0)
+            gather_tokens(2 * e + 1)
+            first_layer(2 * e + 1, 0)
+            permute_w1(e, 1)
+            permute_w1_scales(e, 1)
+            first_layer(2 * e, 1)
+            first_layer(2 * e + 1, 1)
+
+        hq = keep.tile([P, CHUNKS, H_PASSES, CHUNK], U32, name="hq", tag="w1_raw%d" % (E - 1), align_bytes=64)
+        for c in range(4):
+            quantize(c)
+            second_layer(0, c, 0)
+            second_layer(1, c, 0)
+        evacuate(0, 0, 4)
+        for c in range(4, 7):
+            quantize(c)
+            second_layer(0, c, 4)
+            second_layer(1, c, 4)
+        evacuate(0, 4, 7)
+        quantize(7)
+        second_layer(0, 7, 7)
+        evacuate(0, 7, 8)
+        second_layer(1, 7, 4)
+        evacuate(1, 0, 4)
+        evacuate(1, 4, 8)
+        for j in range(2, N_TILES):
+            for first in (0, 4):
+                for c in range(first, first + 4):
+                    second_layer(j, c, first)
+                evacuate(j, first, first + 4)
+
+        last = N_TILES - 1
+        for j in range(last):
+            pick(j, 0, 0, T)
+            if j > 0:
+                combine(j - 1, 0, T)
+            pick(j, 1, 0, T)
+        pick(last, 0, 0, T // 2)
+        combine(last - 1, 0, T)
+        pick(last, 1, 0, T // 2)
+        pick(last, 0, T // 2, T // 2)
+        combine(last, 0, T // 2)
+        pick(last, 1, T // 2, T // 2)
+        combine(last, T // 2, T // 2)

@@ -1,6 +1,7 @@
 from contextlib import ExitStack
 
 import concourse.mybir as mybir
+from concourse.masks import make_identity
 
 K, T, E, C, H, N = 512, 512, 4, 256, 1024, 512
 SLOTS = E * C
@@ -35,7 +36,7 @@ def tile_moe_pkd_mlp_silu_kernel(
     with ExitStack() as ctx:
         keep = ctx.enter_context(tc.tile_pool(name="keep", bufs=1))
         ring = ctx.enter_context(tc.tile_pool(name="ring", bufs=4))
-        pair = ctx.enter_context(tc.tile_pool(name="pair", bufs=4))
+        head = ctx.enter_context(tc.tile_pool(name="head", bufs=1))
         psum = ctx.enter_context(tc.psum_pool(name="psum", bufs=8))
 
         offs_sb = keep.tile([P, SLOTS // GROUP], U16, name="offs_sb")
@@ -44,8 +45,10 @@ def tile_moe_pkd_mlp_silu_kernel(
         xw = keep.tile([P, T], I32, name="xw", align_bytes=64)
         xs = keep.tile([P, T], U8, name="xs", align_bytes=64)
         w1_raw = [keep.tile([P, 2 * H], U8, name="w1_raw%d" % e, tag="w1_raw%d" % e, align_bytes=64) for e in range(E)]
-        w1s_pair = [keep.tile([P, 2, H], U8, name="w1s_pair%d" % i, align_bytes=64) for i in range(E // 2)]
-        w1s_raw = [w1s_pair[e // 2][:, e % 2, :] for e in range(E)]
+        w1s_raw = head.tile([P, H], U8, name="w1s_raw", offset=0, align_bytes=64)
+        xg_first = keep.tile([P, CHUNK], U32, name="xg_first", align_bytes=64)
+        xsg_first = keep.tile([P, CHUNK], U8, name="xsg_first", align_bytes=64)
+        ident = keep.tile([P, P], F32, name="ident")
         w1sp = [keep.tile([P, H], U8, name="w1sp%d" % e, align_bytes=64) for e in range(E)]
         w2w = [keep.tile([P, H_PASSES, 2 * N], U8, name="w2w%d" % e, align_bytes=64) for e in range(E)]
         w2s = keep.tile([P, E * H_PASSES, N], U8, name="w2s", align_bytes=64)
@@ -55,48 +58,52 @@ def tile_moe_pkd_mlp_silu_kernel(
         warm = keep.tile([P, 2], F32, name="warm")
 
         nc.gpsimd.memset(xs[:].bitcast(I32), 0)
-        nc.gpsimd.memset(w1s_pair[0][:].rearrange("p e i -> p (e i)").bitcast(I32), 0)
+        nc.gpsimd.memset(w1s_raw[:].bitcast(I32), 0)
         nc.gpsimd.memset(warm[:, 0:1], 0.0)
-        nc.gpsimd.memset(w1s_pair[1][:].rearrange("p e i -> p (e i)").bitcast(I32), 0)
-        nc.gpsimd.memset(w2s[:].rearrange("p a n -> p (a n)").bitcast(I32), 0)
+        for e in range(1, E):
+            nc.vector.memset(w1sp[e][:].bitcast(I32), 0)
+        nc.vector.memset(w2s[:].rearrange("p a n -> p (a n)").bitcast(I32), 0)
+        make_identity(nc, ident[:])
 
         xs_rows = x_scales[0].rearrange("(q r) t -> r q t", r=4)
-        w1s_rows = w1_scales.rearrange("e s (q r) i -> r q (e s) i", r=4)
         w2s_rows = w2_scales.rearrange("e s (q r) n -> r q (e s) n", r=4)
 
+        def load_x_scales(queue, r):
+            queue.dma_start(xs[r:P:32, :].bitcast(I32), xs_rows[r].bitcast(I32))
+
+        def load_w1_scales(queue, q):
+            queue.dma_start(
+                w1s_raw[32 * q : 32 * q + 4 * E, :].bitcast(I32), w1_scales[:, 0, 4 * q : 4 * q + 4, :].bitcast(I32)
+            )
+
         nc.sync.dma_start(offs_sb[:], offs)
-        nc.sync.dma_start(w1_raw[0][:, 0:H].bitcast(I32), w1_words[0, 0, :, 0:H].bitcast(I32))
+        load_x_scales(nc.scalar, 0)
+        load_x_scales(nc.sync, 1)
+        load_x_scales(nc.scalar, 2)
+        nc.sync.dma_start(w1_raw[0][:].bitcast(I32), w1_words[0, 0].bitcast(I32))
+        load_x_scales(nc.scalar, 3)
         nc.sync.dma_start(xw[:], x_words[0].rearrange("p t r -> p (t r)").bitcast(I32))
-        for r in range(4):
-            nc.scalar.dma_start(xs[r:P:32, :].bitcast(I32), xs_rows[r].bitcast(I32))
-        for r in range(4):
-            queue = nc.scalar if r == 0 else nc.sync
-            queue.dma_start(w1s_pair[0][r:P:32, :, :].bitcast(I32), w1s_rows[r, :, 0:2, :].bitcast(I32))
-        nc.sync.dma_start(w1_raw[0][:, H : 2 * H].bitcast(I32), w1_words[0, 0, :, H : 2 * H].bitcast(I32))
-        nc.sync.dma_start(w1_raw[1][:].bitcast(I32), w1_words[1, 0].bitcast(I32))
-        nc.sync.dma_start(w1_raw[2][:].bitcast(I32), w1_words[2, 0].bitcast(I32))
-        for r in range(4):
-            queue = nc.scalar if r < 2 else nc.sync
-            queue.dma_start(w1s_pair[1][r:P:32, :, :].bitcast(I32), w1s_rows[r, :, 2:4, :].bitcast(I32))
+        for q in range(4):
+            load_w1_scales(nc.scalar if q % 2 == 0 else nc.sync, q)
         nc.scalar.activation(out=warm[:, 1:2], in_=warm[:, 0:1], func=SILU)
-        nc.sync.dma_start(w1_raw[3][:].bitcast(I32), w1_words[3, 0].bitcast(I32))
-        for r in range(4):
-            nc.sync.dma_start(w2s[r:P:32, :, :].bitcast(I32), w2s_rows[r].bitcast(I32))
-        for e in range(E):
-            nc.sync.dma_start(w2w[e][:].bitcast(I32), w2_words[e].rearrange("s p b -> p s b").bitcast(I32))
-        nc.sync.dma_start(pos1_sb[:], pos1)
-        nc.sync.dma_start(pos2_sb[:], pos2)
-        for j in range(N_TILES):
-            nc.sync.dma_start(gates[j][:], gate[:, j * P : (j + 1) * P, :].rearrange("g p t -> p g t"))
+        for e in range(1, E):
+            nc.sync.dma_start(w1_raw[e][:].bitcast(I32), w1_words[e, 0].bitcast(I32))
 
         xg, xsg, w1p = {}, {}, {}
 
-        def gather_tokens(c):
-            entries = offs_sb[:, c * CHUNK // GROUP : (c + 1) * CHUNK // GROUP]
-            xg[c] = pair.tile([P, CHUNK], U32, name="xg", align_bytes=64)
-            xsg[c] = pair.tile([P, CHUNK], U8, name="xsg", align_bytes=64)
-            nc.vector.tensor_copy(xg[c][:], xw[:].bitcast(U32).indirect(entries))
-            nc.vector.tensor_copy(xsg[c][:], xs[:].indirect(entries))
+        def gather_tokens(first, count):
+            entries = offs_sb[:, first * CHUNK // GROUP : (first + count) * CHUNK // GROUP]
+            if first == 0:
+                words = xg_first[:]
+                scales = xsg_first[:]
+            else:
+                cols = slice((first - 1) * CHUNK, (first - 1 + count) * CHUNK)
+                words, scales = xg_rest[:, cols], xsg_rest[:, cols]
+            nc.vector.tensor_copy(words, xw[:].bitcast(U32).indirect(entries))
+            nc.vector.tensor_copy(scales, xs[:].indirect(entries))
+            for i in range(count):
+                xg[first + i] = words[:, i * CHUNK : (i + 1) * CHUNK]
+                xsg[first + i] = scales[:, i * CHUNK : (i + 1) * CHUNK]
 
         def permute_w1(e, s):
             cols = slice(s * K_PASS, (s + 1) * K_PASS)
@@ -106,12 +113,19 @@ def tile_moe_pkd_mlp_silu_kernel(
                 in_=w1_raw[e][:].bitcast(U16)[:, cols].rearrange("p (m t) -> p t m", t=PACK),
             )
 
-        def permute_w1_scales(e, s):
+        def permute_w1_scales(s):
             cols = slice(s * K_PASS, (s + 1) * K_PASS)
             nc.vector.tensor_copy(
-                out=w1sp[e][:, cols].rearrange("p (t m) -> p t m", t=PACK),
-                in_=w1s_raw[e][:, cols].rearrange("p (m t) -> p t m", t=PACK),
+                out=w1sp[0][:, cols].rearrange("p (t m) -> p t m", t=PACK),
+                in_=w1s_raw[:, cols].rearrange("p (m t) -> p t m", t=PACK),
             )
+
+        def shift_w1_scales(e, runs):
+            for first, count in runs:
+                nc.sync.dma_start(
+                    w1sp[e][first : first + count, :].bitcast(I32),
+                    w1sp[0][first + 4 * e : first + 4 * e + count, :].bitcast(I32),
+                )
 
         h_bf = {}
 
@@ -126,18 +140,18 @@ def tile_moe_pkd_mlp_silu_kernel(
                     out=a[:, t, :],
                     lhsT=w1p[(e, s)][:, 2 * t * P : 2 * (t + 1) * P].bitcast(FP4X4),
                     lhsT_scale=w1sp[e][:, col : col + P],
-                    rhs=xg[c][:].bitcast(FP8X4),
-                    rhs_scale=xsg[c][:],
+                    rhs=xg[c].bitcast(FP8X4),
+                    rhs_scale=xsg[c],
                     start=True,
                     stop=True,
                 )
             nc.scalar.activation(out=h_bf[c][:, s, :, :], in_=a[:].rearrange("p t c -> p c t"), func=SILU)
 
-        def quantize(c):
+        def quantize(c, passes=slice(0, H_PASSES)):
             nc.vector.quantize_mx(
-                out=hq[:, c, :, :].rearrange("p s c -> p (s c)").bitcast(FP8X4),
-                scales=hs[:, c, :, :].rearrange("p s c -> p (s c)"),
-                in_=h_bf[c][:].rearrange("p s c t -> p (s c t)"),
+                out=hq[:, c, passes, :].rearrange("p s c -> p (s c)").bitcast(FP8X4),
+                scales=hs[:, c, passes, :].rearrange("p s c -> p (s c)"),
+                in_=h_bf[c][:, passes, :, :].rearrange("p s c t -> p (s c t)"),
             )
 
         banks = {}
@@ -157,8 +171,8 @@ def tile_moe_pkd_mlp_silu_kernel(
                     stop=(s == H_PASSES - 1),
                 )
 
-        def evacuate(j, first, last):
-            nc.scalar.copy(
+        def evacuate(j, first, last, copy=nc.scalar.copy):
+            copy(
                 out=y[j][:, first * CHUNK : last * CHUNK],
                 in_=banks[(j, first)][:, 0 : last - first, :].rearrange("p a c -> p (a c)"),
             )
@@ -186,26 +200,64 @@ def tile_moe_pkd_mlp_silu_kernel(
             nc.vector.tensor_tensor(results[j][:, tokens], picked[j][:, 0, tokens], picked[j][:, 1, tokens], ADD)
             nc.sync.dma_start(out[j * P : (j + 1) * P, tokens], results[j][:, tokens])
 
+        turned_sb = {}
+
+        def add_turned(j, first):
+            turned = psum.tile([P, 2, P], F32, name="turned", tag="bank")
+            for b in range(2):
+                for g in range(2):
+                    nc.tensor.matmul(
+                        turned[:, b, :],
+                        picked[j][:, g, first + b * P : first + (b + 1) * P],
+                        ident[:],
+                        start=(g == 0),
+                        stop=(g == 1),
+                        is_transpose=True,
+                    )
+            turned_sb[(j, first)] = ring.tile([P, 2, P], F32, name="turned_sb")
+            nc.scalar.copy(out=turned_sb[(j, first)][:], in_=turned[:])
+
+        def turn_back(j, first):
+            back = psum.tile([P, 2, P], F32, name="back", tag="bank")
+            for b in range(2):
+                nc.tensor.transpose(back[:, b, :], turned_sb[(j, first)][:, b, :], ident[:])
+            if j not in results:
+                results[j] = ring.tile([P, T], F32, name="result")
+            tokens = slice(first, first + T // 2)
+            nc.scalar.copy(out=results[j][:, tokens], in_=back[:].rearrange("p b t -> p (b t)"))
+
         permute_w1(0, 0)
-        gather_tokens(0)
-        gather_tokens(1)
-        permute_w1_scales(0, 0)
-        first_layer(0, 0)
-        first_layer(1, 0)
         permute_w1(0, 1)
-        permute_w1_scales(0, 1)
+        gather_tokens(0, 1)
+        permute_w1_scales(0)
+        first_layer(0, 0)
+        permute_w1_scales(1)
         first_layer(0, 1)
+        shift_w1_scales(1, [(0, 64), (64, 4), (96, 4)])
+        shift_w1_scales(2, [(0, 112)])
+        shift_w1_scales(3, [(0, 112)])
+
+        for r in range(4):
+            nc.sync.dma_start(w2s[r:P:32, :, :].bitcast(I32), w2s_rows[r].bitcast(I32))
+        for e in range(E):
+            nc.sync.dma_start(w2w[e][:].bitcast(I32), w2_words[e].rearrange("s p b -> p s b").bitcast(I32))
+        nc.sync.dma_start(pos1_sb[:], pos1)
+        nc.sync.dma_start(pos2_sb[:], pos2)
+        for j in range(N_TILES):
+            nc.sync.dma_start(gates[j][:], gate[:, j * P : (j + 1) * P, :].rearrange("g p t -> p g t"))
+
+        xsg_rest = head.tile([P, SLOTS - CHUNK], U8, name="xsg_rest", offset=0, align_bytes=64)
+        xg_rest = head.tile([P, SLOTS - CHUNK], U32, name="xg_rest", offset=SLOTS - CHUNK, align_bytes=64)
+        gather_tokens(1, 1)
+        first_layer(1, 0)
         first_layer(1, 1)
         for e in range(1, E):
-            gather_tokens(2 * e)
+            gather_tokens(2 * e, 2)
             permute_w1(e, 0)
-            permute_w1_scales(e, 0)
             first_layer(2 * e, 0)
-            gather_tokens(2 * e + 1)
-            first_layer(2 * e + 1, 0)
             permute_w1(e, 1)
-            permute_w1_scales(e, 1)
             first_layer(2 * e, 1)
+            first_layer(2 * e + 1, 0)
             first_layer(2 * e + 1, 1)
 
         hq = keep.tile([P, CHUNKS, H_PASSES, CHUNK], U32, name="hq", tag="w1_raw%d" % (E - 1), align_bytes=64)
@@ -213,13 +265,14 @@ def tile_moe_pkd_mlp_silu_kernel(
             quantize(c)
             second_layer(0, c, 0)
             second_layer(1, c, 0)
-        evacuate(0, 0, 4)
+        evacuate(0, 0, 4, nc.vector.tensor_copy)
         for c in range(4, 7):
             quantize(c)
             second_layer(0, c, 4)
             second_layer(1, c, 4)
         evacuate(0, 4, 7)
-        quantize(7)
+        quantize(7, slice(0, 1))
+        quantize(7, slice(1, 2))
         second_layer(0, 7, 7)
         evacuate(0, 7, 8)
         second_layer(1, 7, 4)
@@ -233,14 +286,20 @@ def tile_moe_pkd_mlp_silu_kernel(
 
         last = N_TILES - 1
         for j in range(last):
-            pick(j, 0, 0, T)
-            if j > 0:
-                combine(j - 1, 0, T)
-            pick(j, 1, 0, T)
-        pick(last, 0, 0, T // 2)
-        combine(last - 1, 0, T)
-        pick(last, 1, 0, T // 2)
-        pick(last, 0, T // 2, T // 2)
-        combine(last, 0, T // 2)
-        pick(last, 1, T // 2, T // 2)
-        combine(last, T // 2, T // 2)
+            if j < last - 1:
+                pick(j, 0, 0, T)
+                pick(j, 1, 0, T)
+            for first in (0, T // 2):
+                if j == last - 1:
+                    pick(j, 0, first, T // 2)
+                    pick(j, 1, first, T // 2)
+                add_turned(j, first)
+            for first in (0, T // 2):
+                turn_back(j, first)
+            nc.sync.dma_start(out[j * P : (j + 1) * P, :], results[j][:])
+        pick(last, 0, 0, 384)
+        pick(last, 1, 0, 384)
+        pick(last, 0, 384, 128)
+        combine(last, 0, 384)
+        pick(last, 1, 384, 128)
+        combine(last, 384, 128)

@@ -225,6 +225,7 @@ def tile_moe_pkd_mlp_silu_kernel(
                 results[j] = ring.tile([P, T], F32, name="result")
             tokens = slice(first, first + T // 2)
             nc.scalar.copy(out=results[j][:, tokens], in_=back[:].rearrange("p b t -> p (b t)"))
+            nc.scalar.dma_start(out[j * P : (j + 1) * P, tokens], results[j][:, tokens])
 
         permute_w1(0, 0)
         permute_w1(0, 1)
@@ -296,7 +297,6 @@ def tile_moe_pkd_mlp_silu_kernel(
                 add_turned(j, first)
             for first in (0, T // 2):
                 turn_back(j, first)
-            nc.sync.dma_start(out[j * P : (j + 1) * P, :], results[j][:])
         pick(last, 0, 0, 384)
         pick(last, 1, 0, 384)
         pick(last, 0, 384, 128)

@@ -225,7 +225,6 @@ def tile_moe_pkd_mlp_silu_kernel(
                 results[j] = ring.tile([P, T], F32, name="result")
             tokens = slice(first, first + T // 2)
             nc.scalar.copy(out=results[j][:, tokens], in_=back[:].rearrange("p b t -> p (b t)"))
-            nc.scalar.dma_start(out[j * P : (j + 1) * P, tokens], results[j][:, tokens])
 
         permute_w1(0, 0)
         permute_w1(0, 1)
@@ -297,6 +296,11 @@ def tile_moe_pkd_mlp_silu_kernel(
                 add_turned(j, first)
             for first in (0, T // 2):
                 turn_back(j, first)
+                if j == last - 1:
+                    tokens = slice(first, first + T // 2)
+                    nc.sync.dma_start(out[j * P : (j + 1) * P, tokens], results[j][:, tokens])
+            if j < last - 1:
+                nc.sync.dma_start(out[j * P : (j + 1) * P, :], results[j][:])
         pick(last, 0, 0, 384)
         pick(last, 1, 0, 384)
         pick(last, 0, 384, 128)

@@ -36,26 +36,29 @@ def tile_moe_pkd_mlp_silu_kernel(
     with ExitStack() as ctx:
         keep = ctx.enter_context(tc.tile_pool(name="keep", bufs=1))
         ring = ctx.enter_context(tc.tile_pool(name="ring", bufs=4))
-        head = ctx.enter_context(tc.tile_pool(name="head", bufs=1))
-        psum = ctx.enter_context(tc.psum_pool(name="psum", bufs=8))
+        turn = ctx.enter_context(tc.tile_pool(name="turn", bufs=1))
+        psum = ctx.enter_context(tc.psum_pool(name="psum", bufs=1))
 
         offs_sb = keep.tile([P, SLOTS // GROUP], U16, name="offs_sb")
         pos1_sb = keep.tile([P, T // GROUP], U16, name="pos1_sb")
         pos2_sb = keep.tile([P, T // GROUP], U16, name="pos2_sb")
         xw = keep.tile([P, T], I32, name="xw", align_bytes=64)
         xs = keep.tile([P, T], U8, name="xs", align_bytes=64)
-        w1_raw = [keep.tile([P, 2 * H], U8, name="w1_raw%d" % e, tag="w1_raw%d" % e, align_bytes=64) for e in range(E)]
-        w1s_raw = head.tile([P, H], U8, name="w1s_raw", offset=0, align_bytes=64)
-        xg_first = keep.tile([P, CHUNK], U32, name="xg_first", align_bytes=64)
-        xsg_first = keep.tile([P, CHUNK], U8, name="xsg_first", align_bytes=64)
+        w1s_raw = keep.tile([P, H], U8, name="w1s_raw", align_bytes=64)
         ident = keep.tile([P, P], F32, name="ident")
         w1sp = [keep.tile([P, H], U8, name="w1sp%d" % e, align_bytes=64) for e in range(E)]
         w2w = [keep.tile([P, H_PASSES, 2 * N], U8, name="w2w%d" % e, align_bytes=64) for e in range(E)]
         w2s = keep.tile([P, E * H_PASSES, N], U8, name="w2s", align_bytes=64)
-        gates = [keep.tile([P, 2, T], F32, name="gates%d" % j) for j in range(N_TILES)]
+        gates = keep.tile([P, 2, T], F32, name="gates")
         hs = keep.tile([P, CHUNKS, H_PASSES, CHUNK], U8, name="hs", align_bytes=64)
         y = [keep.tile([P, SLOTS], F32, name="y%d" % j) for j in range(N_TILES)]
         warm = keep.tile([P, 2], F32, name="warm")
+
+        w1_first = keep.tile([P, 2 * K_PASS], U8, name="w1_first", align_bytes=64)
+        w1_second = turn.tile([P, 2 * K_PASS], U8, name="w1_second", offset=0, align_bytes=64)
+        w1_raw = {}
+        for e in range(1, E):
+            w1_raw[e] = turn.tile([P, 2 * H], U8, name="w1_raw%d" % e, offset=2 * H * e, align_bytes=64)
 
         nc.gpsimd.memset(xs[:].bitcast(I32), 0)
         nc.gpsimd.memset(w1s_raw[:].bitcast(I32), 0)
@@ -80,44 +83,44 @@ def tile_moe_pkd_mlp_silu_kernel(
         load_x_scales(nc.scalar, 0)
         load_x_scales(nc.sync, 1)
         load_x_scales(nc.scalar, 2)
-        nc.sync.dma_start(w1_raw[0][:].bitcast(I32), w1_words[0, 0].bitcast(I32))
-        load_x_scales(nc.scalar, 3)
         nc.sync.dma_start(xw[:], x_words[0].rearrange("p t r -> p (t r)").bitcast(I32))
-        for q in range(4):
-            load_w1_scales(nc.scalar if q % 2 == 0 else nc.sync, q)
+        load_x_scales(nc.scalar, 3)
+        nc.sync.dma_start(w1_first[:].bitcast(I32), w1_words[0, 0][:, 0 : 2 * K_PASS].bitcast(I32))
+        load_w1_scales(nc.scalar, 0)
+        load_w1_scales(nc.sync, 1)
+        load_w1_scales(nc.scalar, 2)
+        load_w1_scales(nc.sync, 3)
         nc.scalar.activation(out=warm[:, 1:2], in_=warm[:, 0:1], func=SILU)
-        for e in range(1, E):
-            nc.sync.dma_start(w1_raw[e][:].bitcast(I32), w1_words[e, 0].bitcast(I32))
+        nc.sync.dma_start(w1_second[:].bitcast(I32), w1_words[0, 0][:, 2 * K_PASS : 4 * K_PASS].bitcast(I32))
+        nc.sync.dma_start(w1_raw[1][:].bitcast(I32), w1_words[1, 0].bitcast(I32))
 
         xg, xsg, w1p = {}, {}, {}
 
-        def gather_tokens(first, count):
-            entries = offs_sb[:, first * CHUNK // GROUP : (first + count) * CHUNK // GROUP]
-            if first == 0:
-                words = xg_first[:]
-                scales = xsg_first[:]
-            else:
-                cols = slice((first - 1) * CHUNK, (first - 1 + count) * CHUNK)
-                words, scales = xg_rest[:, cols], xsg_rest[:, cols]
-            nc.vector.tensor_copy(words, xw[:].bitcast(U32).indirect(entries))
-            nc.vector.tensor_copy(scales, xs[:].indirect(entries))
+        def entries(first, count):
+            return offs_sb[:, first * CHUNK // GROUP : (first + count) * CHUNK // GROUP]
+
+        def gather_words(first, count, words):
+            nc.vector.tensor_copy(words, xw[:].bitcast(U32).indirect(entries(first, count)))
             for i in range(count):
                 xg[first + i] = words[:, i * CHUNK : (i + 1) * CHUNK]
+
+        def gather_scales(first, count, scales):
+            nc.vector.tensor_copy(scales, xs[:].indirect(entries(first, count)))
+            for i in range(count):
                 xsg[first + i] = scales[:, i * CHUNK : (i + 1) * CHUNK]
 
-        def permute_w1(e, s):
-            cols = slice(s * K_PASS, (s + 1) * K_PASS)
+        def permute_w1(e, s, raw):
             w1p[(e, s)] = keep.tile([P, 2 * K_PASS], U8, name="w1p%d_%d" % (e, s), align_bytes=64)
             nc.vector.tensor_copy(
                 out=w1p[(e, s)][:].bitcast(U16).rearrange("p (t m) -> p t m", t=PACK),
-                in_=w1_raw[e][:].bitcast(U16)[:, cols].rearrange("p (m t) -> p t m", t=PACK),
+                in_=raw.bitcast(U16).rearrange("p (m t) -> p t m", t=PACK),
             )
 
-        def permute_w1_scales(s):
+        def permute_w1_scales(s, first, count):
             cols = slice(s * K_PASS, (s + 1) * K_PASS)
             nc.vector.tensor_copy(
-                out=w1sp[0][:, cols].rearrange("p (t m) -> p t m", t=PACK),
-                in_=w1s_raw[:, cols].rearrange("p (m t) -> p t m", t=PACK),
+                out=w1sp[0][:, cols].rearrange("p (t m) -> p t m", t=PACK)[:, first : first + count, :],
+                in_=w1s_raw[:, cols].rearrange("p (m t) -> p t m", t=PACK)[:, first : first + count, :],
             )
 
         def shift_w1_scales(e, runs):
@@ -133,7 +136,7 @@ def tile_moe_pkd_mlp_silu_kernel(
             e = c * CHUNK // C
             if c not in h_bf:
                 h_bf[c] = keep.tile([P, H_PASSES, CHUNK, PACK], BF16, name="h_bf%d" % c, align_bytes=64)
-            a = psum.tile([P, PACK, CHUNK], F32, name="a", tag="bank")
+            a = psum.tile([P, PACK, CHUNK], F32, name="a", tag="work", bufs=5)
             for t in range(PACK):
                 col = s * K_PASS + t * P
                 nc.tensor.matmul_mx(
@@ -159,7 +162,7 @@ def tile_moe_pkd_mlp_silu_kernel(
         def second_layer(j, c, first):
             e = c * CHUNK // C
             if (j, first) not in banks:
-                banks[(j, first)] = psum.tile([P, 4, CHUNK], F32, name="yb", tag="bank")
+                banks[(j, first)] = psum.tile([P, 4, CHUNK], F32, name="yb", tag="sums", bufs=3)
             for s in range(H_PASSES):
                 nc.tensor.matmul_mx(
                     out=banks[(j, first)][:, c - first, :],
@@ -187,7 +190,7 @@ def tile_moe_pkd_mlp_silu_kernel(
             nc.vector.tensor_tensor(
                 picked[j][:, g, tokens],
                 y[j][:].indirect(pos[:, first // GROUP : (first + count) // GROUP]),
-                gates[j][:, g, tokens],
+                gates[:, g, tokens],
                 MULT,
             )
 
@@ -203,7 +206,7 @@ def tile_moe_pkd_mlp_silu_kernel(
         turned_sb = {}
 
         def add_turned(j, first):
-            turned = psum.tile([P, 2, P], F32, name="turned", tag="bank")
+            turned = psum.tile([P, 2, P], F32, name="turned", tag="work", bufs=5)
             for b in range(2):
                 for g in range(2):
                     nc.tensor.matmul(
@@ -218,7 +221,7 @@ def tile_moe_pkd_mlp_silu_kernel(
             nc.scalar.copy(out=turned_sb[(j, first)][:], in_=turned[:])
 
         def turn_back(j, first):
-            back = psum.tile([P, 2, P], F32, name="back", tag="bank")
+            back = psum.tile([P, 2, P], F32, name="back", tag="work", bufs=5)
             for b in range(2):
                 nc.tensor.transpose(back[:, b, :], turned_sb[(j, first)][:, b, :], ident[:])
             if j not in results:
@@ -226,59 +229,60 @@ def tile_moe_pkd_mlp_silu_kernel(
             tokens = slice(first, first + T // 2)
             nc.scalar.copy(out=results[j][:, tokens], in_=back[:].rearrange("p b t -> p (b t)"))
 
-        permute_w1(0, 0)
-        permute_w1(0, 1)
-        gather_tokens(0, 1)
-        permute_w1_scales(0)
+        xg_first = keep.tile([P, C], U32, name="xg_first", align_bytes=64)
+        xsg_first = keep.tile([P, C], U8, name="xsg_first", align_bytes=64)
+        gather_words(0, 2, xg_first[:])
+        gather_scales(0, 2, xsg_first[:])
+        permute_w1(0, 0, w1_first[:])
+        permute_w1_scales(0, 0, 2)
+        permute_w1_scales(0, 2, 2)
         first_layer(0, 0)
-        permute_w1_scales(1)
+        permute_w1_scales(1, 0, PACK)
+        first_layer(1, 0)
+        permute_w1(0, 1, w1_second[:])
         first_layer(0, 1)
-        shift_w1_scales(1, [(0, 64), (64, 4), (96, 4)])
-        shift_w1_scales(2, [(0, 112)])
-        shift_w1_scales(3, [(0, 112)])
+        first_layer(1, 1)
 
+        shift_w1_scales(1, [(0, 64), (64, 4), (96, 4)])
+        nc.sync.dma_start(w1_raw[2][:].bitcast(I32), w1_words[2, 0].bitcast(I32))
+        shift_w1_scales(2, [(0, 112)])
+        nc.sync.dma_start(w1_raw[3][:].bitcast(I32), w1_words[3, 0].bitcast(I32))
+        shift_w1_scales(3, [(0, 112)])
         for r in range(4):
             nc.sync.dma_start(w2s[r:P:32, :, :].bitcast(I32), w2s_rows[r].bitcast(I32))
         for e in range(E):
             nc.sync.dma_start(w2w[e][:].bitcast(I32), w2_words[e].rearrange("s p b -> p s b").bitcast(I32))
         nc.sync.dma_start(pos1_sb[:], pos1)
         nc.sync.dma_start(pos2_sb[:], pos2)
-        for j in range(N_TILES):
-            nc.sync.dma_start(gates[j][:], gate[:, j * P : (j + 1) * P, :].rearrange("g p t -> p g t"))
+        nc.sync.dma_start(gates[:], gate[:, 0:P, :].rearrange("g p t -> p g t"))
 
-        xsg_rest = head.tile([P, SLOTS - CHUNK], U8, name="xsg_rest", offset=0, align_bytes=64)
-        xg_rest = head.tile([P, SLOTS - CHUNK], U32, name="xg_rest", offset=SLOTS - CHUNK, align_bytes=64)
-        gather_tokens(1, 1)
-        first_layer(1, 0)
-        first_layer(1, 1)
         for e in range(1, E):
-            gather_tokens(2 * e, 2)
-            permute_w1(e, 0)
+            base = 2 * H * (e - 1)
+            scales = turn.tile([P, C], U8, name="xsg%d" % e, offset=base, align_bytes=64)
+            words = turn.tile([P, C], U32, name="xg%d" % e, offset=base + C, align_bytes=64)
+            permute_w1(e, 0, w1_raw[e][:, 0 : 2 * K_PASS])
+            gather_words(2 * e, 2, words[:])
+            gather_scales(2 * e, 2, scales[:])
             first_layer(2 * e, 0)
-            permute_w1(e, 1)
+            permute_w1(e, 1, w1_raw[e][:, 2 * K_PASS : 4 * K_PASS])
             first_layer(2 * e, 1)
             first_layer(2 * e + 1, 0)
             first_layer(2 * e + 1, 1)
 
-        hq = keep.tile([P, CHUNKS, H_PASSES, CHUNK], U32, name="hq", tag="w1_raw%d" % (E - 1), align_bytes=64)
+        hq = turn.tile([P, CHUNKS, H_PASSES, CHUNK], U32, name="hq", offset=2 * H * (E - 1), align_bytes=64)
         for c in range(4):
             quantize(c)
             second_layer(0, c, 0)
-            second_layer(1, c, 0)
-        evacuate(0, 0, 4, nc.vector.tensor_copy)
         for c in range(4, 7):
             quantize(c)
             second_layer(0, c, 4)
-            second_layer(1, c, 4)
-        evacuate(0, 4, 7)
         quantize(7, slice(0, 1))
         quantize(7, slice(1, 2))
         second_layer(0, 7, 7)
+        evacuate(0, 0, 4)
+        evacuate(0, 4, 7, nc.vector.tensor_copy)
         evacuate(0, 7, 8)
-        second_layer(1, 7, 4)
-        evacuate(1, 0, 4)
-        evacuate(1, 4, 8)
-        for j in range(2, N_TILES):
+        for j in range(1, N_TILES):
             for first in (0, 4):
                 for c in range(first, first + 4):
                     second_layer(j, c, first)

@@ -52,7 +52,6 @@ def tile_moe_pkd_mlp_silu_kernel(
         gates = keep.tile([P, 2, T], F32, name="gates")
         hs = keep.tile([P, CHUNKS, H_PASSES, CHUNK], U8, name="hs", align_bytes=64)
         y = [keep.tile([P, SLOTS], F32, name="y%d" % j) for j in range(N_TILES)]
-        warm = keep.tile([P, 2], F32, name="warm")
 
         w1_first = keep.tile([P, 2 * K_PASS], U8, name="w1_first", align_bytes=64)
         w1_second = turn.tile([P, 2 * K_PASS], U8, name="w1_second", offset=0, align_bytes=64)
@@ -62,7 +61,6 @@ def tile_moe_pkd_mlp_silu_kernel(
 
         nc.gpsimd.memset(xs[:].bitcast(I32), 0)
         nc.gpsimd.memset(w1s_raw[:].bitcast(I32), 0)
-        nc.gpsimd.memset(warm[:, 0:1], 0.0)
         for e in range(1, E):
             nc.vector.memset(w1sp[e][:].bitcast(I32), 0)
         nc.vector.memset(w2s[:].rearrange("p a n -> p (a n)").bitcast(I32), 0)
@@ -90,7 +88,6 @@ def tile_moe_pkd_mlp_silu_kernel(
         load_w1_scales(nc.sync, 1)
         load_w1_scales(nc.scalar, 2)
         load_w1_scales(nc.sync, 3)
-        nc.scalar.activation(out=warm[:, 1:2], in_=warm[:, 0:1], func=SILU)
         nc.sync.dma_start(w1_second[:].bitcast(I32), w1_words[0, 0][:, 2 * K_PASS : 4 * K_PASS].bitcast(I32))
         nc.sync.dma_start(w1_raw[1][:].bitcast(I32), w1_words[1, 0].bitcast(I32))
 

@@ -89,7 +89,8 @@ def tile_moe_pkd_mlp_silu_kernel(
         load_w1_scales(nc.scalar, 2)
         load_w1_scales(nc.sync, 3)
         nc.sync.dma_start(w1_second[:].bitcast(I32), w1_words[0, 0][:, 2 * K_PASS : 4 * K_PASS].bitcast(I32))
-        nc.sync.dma_start(w1_raw[1][:].bitcast(I32), w1_words[1, 0].bitcast(I32))
+        for e in range(1, E):
+            nc.sync.dma_start(w1_raw[e][:].bitcast(I32), w1_words[e, 0].bitcast(I32))
 
         xg, xsg, w1p = {}, {}, {}
 
@@ -203,7 +204,7 @@ def tile_moe_pkd_mlp_silu_kernel(
         turned_sb = {}
 
         def add_turned(j, first):
-            turned = psum.tile([P, 2, P], F32, name="turned", tag="work", bufs=5)
+            turned = psum.tile([P, 2, P], F32, name="turned", tag="sums", bufs=3)
             for b in range(2):
                 for g in range(2):
                     nc.tensor.matmul(
@@ -241,9 +242,7 @@ def tile_moe_pkd_mlp_silu_kernel(
         first_layer(1, 1)
 
         shift_w1_scales(1, [(0, 64), (64, 4), (96, 4)])
-        nc.sync.dma_start(w1_raw[2][:].bitcast(I32), w1_words[2, 0].bitcast(I32))
         shift_w1_scales(2, [(0, 112)])
-        nc.sync.dma_start(w1_raw[3][:].bitcast(I32), w1_words[3, 0].bitcast(I32))
         shift_w1_scales(3, [(0, 112)])
         for r in range(4):
             nc.sync.dma_start(w2s[r:P:32, :, :].bitcast(I32), w2s_rows[r].bitcast(I32))

@@ -59,18 +59,17 @@ def tile_moe_pkd_mlp_silu_kernel(
         for e in range(1, E):
             w1_raw[e] = turn.tile([P, 2 * H], U8, name="w1_raw%d" % e, offset=2 * H * e, align_bytes=64)
 
-        nc.gpsimd.memset(xs[:].bitcast(I32), 0)
         nc.gpsimd.memset(w1s_raw[:].bitcast(I32), 0)
         for e in range(1, E):
-            nc.vector.memset(w1sp[e][:].bitcast(I32), 0)
+            nc.vector.memset(w1sp[e][96:P, :].bitcast(I32), 0)
         nc.vector.memset(w2s[:].rearrange("p a n -> p (a n)").bitcast(I32), 0)
         make_identity(nc, ident[:])
 
-        xs_rows = x_scales[0].rearrange("(q r) t -> r q t", r=4)
         w2s_rows = w2_scales.rearrange("e s (q r) n -> r q (e s) n", r=4)
 
-        def load_x_scales(queue, r):
-            queue.dma_start(xs[r:P:32, :].bitcast(I32), xs_rows[r].bitcast(I32))
+        def load_x_scales(queue, q):
+            rows = x_scales[0, 4 * q : 4 * q + 4, :].bitcast(I32)
+            queue.dma_start(xs[32 * q : 32 * q + 32, :].bitcast(I32), rows.unsqueeze(0).to_broadcast([8, 4, T // 4]))
 
         def load_w1_scales(queue, q):
             queue.dma_start(
@@ -81,13 +80,12 @@ def tile_moe_pkd_mlp_silu_kernel(
         load_x_scales(nc.scalar, 0)
         load_x_scales(nc.sync, 1)
         load_x_scales(nc.scalar, 2)
+        load_x_scales(nc.sync, 3)
+        nc.scalar.dma_start(w1_first[:].bitcast(I32), w1_words[0, 0][:, 0 : 2 * K_PASS].bitcast(I32))
         nc.sync.dma_start(xw[:], x_words[0].rearrange("p t r -> p (t r)").bitcast(I32))
-        load_x_scales(nc.scalar, 3)
-        nc.sync.dma_start(w1_first[:].bitcast(I32), w1_words[0, 0][:, 0 : 2 * K_PASS].bitcast(I32))
         load_w1_scales(nc.scalar, 0)
-        load_w1_scales(nc.sync, 1)
-        load_w1_scales(nc.scalar, 2)
-        load_w1_scales(nc.sync, 3)
+        for q in range(1, 4):
+            load_w1_scales(nc.sync, q)
         nc.sync.dma_start(w1_second[:].bitcast(I32), w1_words[0, 0][:, 2 * K_PASS : 4 * K_PASS].bitcast(I32))
         for e in range(1, E):
             nc.sync.dma_start(w1_raw[e][:].bitcast(I32), w1_words[e, 0].bitcast(I32))
@@ -121,11 +119,11 @@ def tile_moe_pkd_mlp_silu_kernel(
                 in_=w1s_raw[:, cols].rearrange("p (m t) -> p t m", t=PACK)[:, first : first + count, :],
             )
 
-        def shift_w1_scales(e, runs):
-            for first, count in runs:
+        def shift_w1_scales(e, cols=slice(0, H)):
+            for first, count in ((0, 64), (64, 32), (96, 4)):
                 nc.sync.dma_start(
-                    w1sp[e][first : first + count, :].bitcast(I32),
-                    w1sp[0][first + 4 * e : first + 4 * e + count, :].bitcast(I32),
+                    w1sp[e][first : first + count, cols].bitcast(I32),
+                    w1sp[0][first + 4 * e : first + 4 * e + count, cols].bitcast(I32),
                 )
 
         h_bf = {}
@@ -228,9 +226,9 @@ def tile_moe_pkd_mlp_silu_kernel(
             nc.scalar.copy(out=results[j][:, tokens], in_=back[:].rearrange("p b t -> p (b t)"))
 
         xg_first = keep.tile([P, C], U32, name="xg_first", align_bytes=64)
-        xsg_first = keep.tile([P, C], U8, name="xsg_first", align_bytes=64)
+        xsg_first = keep.tile([P, 3 * CHUNK], U8, name="xsg_first", align_bytes=64)
+        gather_scales(0, 3, xsg_first[:])
         gather_words(0, 2, xg_first[:])
-        gather_scales(0, 2, xsg_first[:])
         permute_w1(0, 0, w1_first[:])
         permute_w1_scales(0, 0, 2)
         permute_w1_scales(0, 2, 2)
@@ -241,9 +239,10 @@ def tile_moe_pkd_mlp_silu_kernel(
         first_layer(0, 1)
         first_layer(1, 1)
 
-        shift_w1_scales(1, [(0, 64), (64, 4), (96, 4)])
-        shift_w1_scales(2, [(0, 112)])
-        shift_w1_scales(3, [(0, 112)])
+        for s in range(H_PASSES):
+            shift_w1_scales(1, slice(s * K_PASS, (s + 1) * K_PASS))
+        for e in range(2, E):
+            shift_w1_scales(e)
         for r in range(4):
             nc.sync.dma_start(w2s[r:P:32, :, :].bitcast(I32), w2s_rows[r].bitcast(I32))
         for e in range(E):
@@ -258,7 +257,10 @@ def tile_moe_pkd_mlp_silu_kernel(
             words = turn.tile([P, C], U32, name="xg%d" % e, offset=base + C, align_bytes=64)
             permute_w1(e, 0, w1_raw[e][:, 0 : 2 * K_PASS])
             gather_words(2 * e, 2, words[:])
-            gather_scales(2 * e, 2, scales[:])
+            if e == 1:
+                gather_scales(3, 1, scales[:, 0:CHUNK])
+            else:
+                gather_scales(2 * e, 2, scales[:])
             first_layer(2 * e, 0)
             permute_w1(e, 1, w1_raw[e][:, 2 * K_PASS : 4 * K_PASS])
             first_layer(2 * e, 1)

@@ -23,6 +23,7 @@ U8 = mybir.dt.uint8
 FP8X4 = mybir.dt.float8_e4m3fn_x4
 FP4X4 = mybir.dt.float4_e2m1fn_x4
 SILU = mybir.ActivationFunctionType.Silu
+COPY = mybir.ActivationFunctionType.Copy
 MULT = mybir.AluOpType.mult
 ADD = mybir.AluOpType.add
 
@@ -50,6 +51,7 @@ def tile_moe_pkd_mlp_silu_kernel(
         w2w = [keep.tile([P, H_PASSES, 2 * N], U8, name="w2w%d" % e, align_bytes=64) for e in range(E)]
         w2s = keep.tile([P, E * H_PASSES, N], U8, name="w2s", align_bytes=64)
         gates = keep.tile([P, 2, T], F32, name="gates")
+        gate_cols = keep.tile([P, T // P], F32, name="gate_cols")
         hs = keep.tile([P, CHUNKS, H_PASSES, CHUNK], U8, name="hs", align_bytes=64)
         y = [keep.tile([P, SLOTS], F32, name="y%d" % j) for j in range(N_TILES)]
 
@@ -126,13 +128,18 @@ def tile_moe_pkd_mlp_silu_kernel(
                     w1sp[0][first + 4 * e : first + 4 * e + count, cols].bitcast(I32),
                 )
 
+        def bank(b, shape, name):
+            return psum.tile(shape, F32, name=name, tag="bank%d" % b)
+
         h_bf = {}
+        groups = []
 
         def first_layer(c, s):
             e = c * CHUNK // C
             if c not in h_bf:
                 h_bf[c] = keep.tile([P, H_PASSES, CHUNK, PACK], BF16, name="h_bf%d" % c, align_bytes=64)
-            a = psum.tile([P, PACK, CHUNK], F32, name="a", tag="work", bufs=5)
+            a = bank(len(groups) % 8, [P, PACK, CHUNK], "a")
+            groups.append(a)
             for t in range(PACK):
                 col = s * K_PASS + t * P
                 nc.tensor.matmul_mx(
@@ -154,11 +161,12 @@ def tile_moe_pkd_mlp_silu_kernel(
             )
 
         banks = {}
+        sum_bank = {(0, 0): 0, (0, 4): 1, (1, 0): 2, (1, 4): 3, (0, 7): 4, (2, 0): 0, (2, 4): 1, (3, 0): 4, (3, 4): 2}
 
         def second_layer(j, c, first):
             e = c * CHUNK // C
             if (j, first) not in banks:
-                banks[(j, first)] = psum.tile([P, 4, CHUNK], F32, name="yb", tag="sums", bufs=3)
+                banks[(j, first)] = bank(sum_bank[(j, first)], [P, 4, CHUNK], "yb")
             for s in range(H_PASSES):
                 nc.tensor.matmul_mx(
                     out=banks[(j, first)][:, c - first, :],
@@ -190,40 +198,42 @@ def tile_moe_pkd_mlp_silu_kernel(
                 MULT,
             )
 
+        def fetch(j, blocks=4):
+            if j not in picked:
+                picked[j] = ring.tile([P, 2, T], F32, name="picked")
+            nc.scalar.activation(
+                picked[j][:, 0, 0 : blocks * P], y[j][:].indirect(pos1_sb[:, 0 : blocks * P // GROUP]), COPY
+            )
+
+        turned, scaled, back = {}, {}, {}
+
+        def turn_over(j, blocks=4):
+            turned[j] = bank(5 + j, [P, T // P, P], "turned")
+            for b in range(blocks):
+                nc.tensor.transpose(turned[j][:, b, :], picked[j][:, 0, b * P : (b + 1) * P], ident[:])
+
+        def weigh(j, blocks=4):
+            scaled[j] = ring.tile([P, T // P, P], F32, name="scaled")
+            for b in range(blocks):
+                nc.scalar.activation(scaled[j][:, b, :], turned[j][:, b, :], COPY, scale=gate_cols[:, b : b + 1])
+
+        def turn_back(j, first, count, b0):
+            back[(j, first)] = bank(b0, [P, T], "back")
+            for b in range(first // P, (first + count) // P):
+                nc.tensor.transpose(back[(j, first)][:, b * P : (b + 1) * P], scaled[j][:, b, :], ident[:])
+
         results = {}
 
-        def combine(j, first, count):
+        def add(j, first, count):
             tokens = slice(first, first + count)
             if j not in results:
                 results[j] = ring.tile([P, T], F32, name="result")
-            nc.vector.tensor_tensor(results[j][:, tokens], picked[j][:, 0, tokens], picked[j][:, 1, tokens], ADD)
+            weighted = back[(j, first)][:, tokens] if (j, first) in back else picked[j][:, 0, tokens]
+            nc.vector.tensor_tensor(results[j][:, tokens], weighted, picked[j][:, 1, tokens], ADD)
+
+        def store(j, first, count):
+            tokens = slice(first, first + count)
             nc.sync.dma_start(out[j * P : (j + 1) * P, tokens], results[j][:, tokens])
-
-        turned_sb = {}
-
-        def add_turned(j, first):
-            turned = psum.tile([P, 2, P], F32, name="turned", tag="sums", bufs=3)
-            for b in range(2):
-                for g in range(2):
-                    nc.tensor.matmul(
-                        turned[:, b, :],
-                        picked[j][:, g, first + b * P : first + (b + 1) * P],
-                        ident[:],
-                        start=(g == 0),
-                        stop=(g == 1),
-                        is_transpose=True,
-                    )
-            turned_sb[(j, first)] = ring.tile([P, 2, P], F32, name="turned_sb")
-            nc.scalar.copy(out=turned_sb[(j, first)][:], in_=turned[:])
-
-        def turn_back(j, first):
-            back = psum.tile([P, 2, P], F32, name="back", tag="work", bufs=5)
-            for b in range(2):
-                nc.tensor.transpose(back[:, b, :], turned_sb[(j, first)][:, b, :], ident[:])
-            if j not in results:
-                results[j] = ring.tile([P, T], F32, name="result")
-            tokens = slice(first, first + T // 2)
-            nc.scalar.copy(out=results[j][:, tokens], in_=back[:].rearrange("p b t -> p (b t)"))
 
         xg_first = keep.tile([P, C], U32, name="xg_first", align_bytes=64)
         xsg_first = keep.tile([P, 3 * CHUNK], U8, name="xsg_first", align_bytes=64)
@@ -250,6 +260,8 @@ def tile_moe_pkd_mlp_silu_kernel(
         nc.sync.dma_start(pos1_sb[:], pos1)
         nc.sync.dma_start(pos2_sb[:], pos2)
         nc.sync.dma_start(gates[:], gate[:, 0:P, :].rearrange("g p t -> p g t"))
+        with nc.allow_non_contiguous_dma(reason="one weight a partition"):
+            nc.sync.dma_start(gate_cols[:], gate[0, 0, :].rearrange("(b p) -> p b", p=P))
 
         for e in range(1, E):
             base = 2 * H * (e - 1)
@@ -280,32 +292,40 @@ def tile_moe_pkd_mlp_silu_kernel(
         evacuate(0, 0, 4)
         evacuate(0, 4, 7, nc.vector.tensor_copy)
         evacuate(0, 7, 8)
-        for j in range(1, N_TILES):
+
+        def sums(j):
             for first in (0, 4):
                 for c in range(first, first + 4):
                     second_layer(j, c, first)
-                evacuate(j, first, first + 4)
 
-        last = N_TILES - 1
-        for j in range(last):
-            if j < last - 1:
-                pick(j, 0, 0, T)
-                pick(j, 1, 0, T)
-            for first in (0, T // 2):
-                if j == last - 1:
-                    pick(j, 0, first, T // 2)
-                    pick(j, 1, first, T // 2)
-                add_turned(j, first)
-            for first in (0, T // 2):
-                turn_back(j, first)
-                if j == last - 1:
-                    tokens = slice(first, first + T // 2)
-                    nc.sync.dma_start(out[j * P : (j + 1) * P, tokens], results[j][:, tokens])
-            if j < last - 1:
-                nc.sync.dma_start(out[j * P : (j + 1) * P, :], results[j][:])
-        pick(last, 0, 0, 384)
-        pick(last, 1, 0, 384)
-        pick(last, 0, 384, 128)
-        combine(last, 0, 384)
-        pick(last, 1, 384, 128)
-        combine(last, 384, 128)
+        most = T - P
+        for j in range(1, N_TILES):
+            sums(j)
+            evacuate(j, 0, 4, nc.vector.tensor_copy if j == 1 else nc.scalar.copy)
+            evacuate(j, 4, 8)
+        for j in range(N_TILES):
+            pick(j, 1, 0, T)
+        fetch(0)
+        turn_over(0)
+        fetch(1)
+        turn_over(1)
+        pick(3, 0, 0, T)
+        weigh(0)
+        turn_back(0, 0, T, 3)
+        fetch(2, 3)
+        turn_over(2, 3)
+        pick(2, 0, most, P)
+        add(3, 0, T)
+        store(3, 0, T)
+        weigh(1)
+        turn_back(1, 0, T, 0)
+        add(0, 0, T)
+        store(0, 0, T)
+        weigh(2, 3)
+        turn_back(2, 0, most, 1)
+        add(2, most, P)
+        store(2, most, P)
+        add(1, 0, T)
+        store(1, 0, T)
+        add(2, 0, most)
+        store(2, 0, most)

@@ -52,7 +52,7 @@ def tile_moe_pkd_mlp_silu_kernel(
         w2s = keep.tile([P, E * H_PASSES, N], U8, name="w2s", align_bytes=64)
         gates = keep.tile([P, 2, T], F32, name="gates")
         gate_cols = keep.tile([P, T // P], F32, name="gate_cols")
-        hs = keep.tile([P, CHUNKS, H_PASSES, CHUNK], U8, name="hs", align_bytes=64)
+        hs = keep.tile([P, E, H_PASSES, C], U8, name="hs", align_bytes=64)
         y = [keep.tile([P, SLOTS], F32, name="y%d" % j) for j in range(N_TILES)]
 
         w1_first = keep.tile([P, 2 * K_PASS], U8, name="w1_first", align_bytes=64)
@@ -136,8 +136,9 @@ def tile_moe_pkd_mlp_silu_kernel(
 
         def first_layer(c, s):
             e = c * CHUNK // C
-            if c not in h_bf:
-                h_bf[c] = keep.tile([P, H_PASSES, CHUNK, PACK], BF16, name="h_bf%d" % c, align_bytes=64)
+            if (e, s) not in h_bf:
+                h_bf[(e, s)] = keep.tile([P, C, PACK], BF16, name="h_bf%d_%d" % (e, s), align_bytes=64)
+            place = c * CHUNK - e * C
             a = bank(len(groups) % 8, [P, PACK, CHUNK], "a")
             groups.append(a)
             for t in range(PACK):
@@ -151,29 +152,30 @@ def tile_moe_pkd_mlp_silu_kernel(
                     start=True,
                     stop=True,
                 )
-            nc.scalar.activation(out=h_bf[c][:, s, :, :], in_=a[:].rearrange("p t c -> p c t"), func=SILU)
+            nc.scalar.activation(out=h_bf[(e, s)][:, place : place + CHUNK, :], in_=a[:].rearrange("p t c -> p c t"), func=SILU)
 
-        def quantize(c, passes=slice(0, H_PASSES)):
+        def quantize(e, s, places=slice(0, C)):
             nc.vector.quantize_mx(
-                out=hq[:, c, passes, :].rearrange("p s c -> p (s c)").bitcast(FP8X4),
-                scales=hs[:, c, passes, :].rearrange("p s c -> p (s c)"),
-                in_=h_bf[c][:, passes, :, :].rearrange("p s c t -> p (s c t)"),
+                out=hq[:, e, s, places].bitcast(FP8X4),
+                scales=hs[:, e, s, places],
+                in_=h_bf[(e, s)][:, places, :].rearrange("p c t -> p (c t)"),
             )
 
         banks = {}
-        sum_bank = {(0, 0): 0, (0, 4): 1, (1, 0): 2, (1, 4): 3, (0, 7): 4, (2, 0): 0, (2, 4): 1, (3, 0): 4, (3, 4): 2}
+        sum_bank = {(0, 0): 0, (0, 4): 1, (1, 0): 2, (1, 4): 3, (0, 7): 4, (2, 0): 5, (2, 4): 6, (3, 0): 0, (3, 4): 7}
 
-        def second_layer(j, c, first):
+        def second_layer(j, c, first, count=2):
             e = c * CHUNK // C
+            places = slice(c * CHUNK - e * C, (c + count) * CHUNK - e * C)
             if (j, first) not in banks:
-                banks[(j, first)] = bank(sum_bank[(j, first)], [P, 4, CHUNK], "yb")
+                banks[(j, first)] = bank(sum_bank[(j, first)], [P, 4 * CHUNK], "yb")
             for s in range(H_PASSES):
                 nc.tensor.matmul_mx(
-                    out=banks[(j, first)][:, c - first, :],
+                    out=banks[(j, first)][:, (c - first) * CHUNK : (c - first + count) * CHUNK],
                     lhsT=w2w[e][:, s, 2 * j * P : 2 * (j + 1) * P].bitcast(FP4X4),
                     lhsT_scale=w2s[:, e * H_PASSES + s, j * P : (j + 1) * P],
-                    rhs=hq[:, c, s, :].bitcast(FP8X4),
-                    rhs_scale=hs[:, c, s, :],
+                    rhs=hq[:, e, s, places].bitcast(FP8X4),
+                    rhs_scale=hs[:, e, s, places],
                     start=(s == 0),
                     stop=(s == H_PASSES - 1),
                 )
@@ -181,7 +183,7 @@ def tile_moe_pkd_mlp_silu_kernel(
         def evacuate(j, first, last, copy=nc.scalar.copy):
             copy(
                 out=y[j][:, first * CHUNK : last * CHUNK],
-                in_=banks[(j, first)][:, 0 : last - first, :].rearrange("p a c -> p (a c)"),
+                in_=banks[(j, first)][:, 0 : (last - first) * CHUNK],
             )
 
         picked = {}
@@ -198,19 +200,20 @@ def tile_moe_pkd_mlp_silu_kernel(
                 MULT,
             )
 
+        fetched = {}
+
         def fetch(j, blocks=4):
-            if j not in picked:
-                picked[j] = ring.tile([P, 2, T], F32, name="picked")
+            fetched[j] = turn.tile([P, T], F32, name="fetched%d" % j, offset=2 * H * (E - 1) + 4 * T * j, align_bytes=64)
             nc.scalar.activation(
-                picked[j][:, 0, 0 : blocks * P], y[j][:].indirect(pos1_sb[:, 0 : blocks * P // GROUP]), COPY
+                fetched[j][:, 0 : blocks * P], y[j][:].indirect(pos1_sb[:, 0 : blocks * P // GROUP]), COPY
             )
 
         turned, scaled, back = {}, {}, {}
 
         def turn_over(j, blocks=4):
-            turned[j] = bank(5 + j, [P, T // P, P], "turned")
+            turned[j] = bank((1, 2, 4)[j], [P, T // P, P], "turned")
             for b in range(blocks):
-                nc.tensor.transpose(turned[j][:, b, :], picked[j][:, 0, b * P : (b + 1) * P], ident[:])
+                nc.tensor.transpose(turned[j][:, b, :], fetched[j][:, b * P : (b + 1) * P], ident[:])
 
         def weigh(j, blocks=4):
             scaled[j] = ring.tile([P, T // P, P], F32, name="scaled")
@@ -274,28 +277,28 @@ def tile_moe_pkd_mlp_silu_kernel(
             else:
                 gather_scales(2 * e, 2, scales[:])
             first_layer(2 * e, 0)
+            first_layer(2 * e + 1, 0)
             permute_w1(e, 1, w1_raw[e][:, 2 * K_PASS : 4 * K_PASS])
             first_layer(2 * e, 1)
-            first_layer(2 * e + 1, 0)
             first_layer(2 * e + 1, 1)
 
-        hq = turn.tile([P, CHUNKS, H_PASSES, CHUNK], U32, name="hq", offset=2 * H * (E - 1), align_bytes=64)
-        for c in range(4):
-            quantize(c)
-            second_layer(0, c, 0)
-        for c in range(4, 7):
-            quantize(c)
-            second_layer(0, c, 4)
-        quantize(7, slice(0, 1))
-        quantize(7, slice(1, 2))
-        second_layer(0, 7, 7)
+        hq = turn.tile([P, E, H_PASSES, C], U32, name="hq", offset=2 * H * (E - 1), align_bytes=64)
+        for e in range(E - 1):
+            quantize(e, 0)
+            quantize(e, 1)
+            second_layer(0, 2 * e, 4 * (e // 2))
+        quantize(3, 0)
+        quantize(3, 1, slice(0, CHUNK))
+        second_layer(0, 6, 4, 1)
+        quantize(3, 1, slice(CHUNK, C))
+        second_layer(0, 7, 7, 1)
         evacuate(0, 0, 4)
         evacuate(0, 4, 7, nc.vector.tensor_copy)
         evacuate(0, 7, 8)
 
         def sums(j):
             for first in (0, 4):
-                for c in range(first, first + 4):
+                for c in (first, first + 2):
                     second_layer(j, c, first)
 
         most = T - P
@@ -318,14 +321,17 @@ def tile_moe_pkd_mlp_silu_kernel(
         add(3, 0, T)
         store(3, 0, T)
         weigh(1)
-        turn_back(1, 0, T, 0)
+        turn_back(1, 0, T, 5)
+        add(2, most, P)
+        store(2, most, P)
         add(0, 0, T)
         store(0, 0, T)
         weigh(2, 3)
-        turn_back(2, 0, most, 1)
-        add(2, most, P)
-        store(2, most, P)
+        turn_back(2, 0, 2 * P, 6)
+        turn_back(2, 2 * P, P, 7)
         add(1, 0, T)
         store(1, 0, T)
-        add(2, 0, most)
-        store(2, 0, most)
+        add(2, 0, 2 * P)
+        store(2, 0, 2 * P)
+        add(2, 2 * P, P)
+        store(2, 2 * P, P)

@@ -45,7 +45,6 @@ def tile_moe_pkd_mlp_silu_kernel(
         pos2_sb = keep.tile([P, T // GROUP], U16, name="pos2_sb")
         xw = keep.tile([P, T], I32, name="xw", align_bytes=64)
         xs = keep.tile([P, T], U8, name="xs", align_bytes=64)
-        w1s_raw = keep.tile([P, H], U8, name="w1s_raw", align_bytes=64)
         ident = keep.tile([P, P], F32, name="ident")
         w1sp = [keep.tile([P, H], U8, name="w1sp%d" % e, align_bytes=64) for e in range(E)]
         w2w = [keep.tile([P, H_PASSES, 2 * N], U8, name="w2w%d" % e, align_bytes=64) for e in range(E)]
@@ -55,13 +54,16 @@ def tile_moe_pkd_mlp_silu_kernel(
         hs = keep.tile([P, E, H_PASSES, C], U8, name="hs", align_bytes=64)
         y = [keep.tile([P, SLOTS], F32, name="y%d" % j) for j in range(N_TILES)]
 
-        w1_first = keep.tile([P, 2 * K_PASS], U8, name="w1_first", align_bytes=64)
-        w1_second = turn.tile([P, 2 * K_PASS], U8, name="w1_second", offset=0, align_bytes=64)
+        w1_zero = keep.tile([P, 2 * H], U8, name="w1_zero", align_bytes=64)
+        held = turn.tile([P, H], U8, name="held", offset=0, align_bytes=64)
+        warm = keep.tile([P, 2], F32, name="warm")
         w1_raw = {}
         for e in range(1, E):
             w1_raw[e] = turn.tile([P, 2 * H], U8, name="w1_raw%d" % e, offset=2 * H * e, align_bytes=64)
 
+        w1s_raw = held
         nc.gpsimd.memset(w1s_raw[:].bitcast(I32), 0)
+        nc.vector.memset(warm[:, 0:1], 0.0)
         for e in range(1, E):
             nc.vector.memset(w1sp[e][96:P, :].bitcast(I32), 0)
         nc.vector.memset(w2s[:].rearrange("p a n -> p (a n)").bitcast(I32), 0)
@@ -83,12 +85,12 @@ def tile_moe_pkd_mlp_silu_kernel(
         load_x_scales(nc.sync, 1)
         load_x_scales(nc.scalar, 2)
         load_x_scales(nc.sync, 3)
-        nc.scalar.dma_start(w1_first[:].bitcast(I32), w1_words[0, 0][:, 0 : 2 * K_PASS].bitcast(I32))
+        nc.scalar.dma_start(w1_zero[:].bitcast(I32), w1_words[0, 0].bitcast(I32))
         nc.sync.dma_start(xw[:], x_words[0].rearrange("p t r -> p (t r)").bitcast(I32))
         load_w1_scales(nc.scalar, 0)
         for q in range(1, 4):
             load_w1_scales(nc.sync, q)
-        nc.sync.dma_start(w1_second[:].bitcast(I32), w1_words[0, 0][:, 2 * K_PASS : 4 * K_PASS].bitcast(I32))
+        nc.scalar.activation(out=warm[:, 1:2], in_=warm[:, 0:1], func=SILU)
         for e in range(1, E):
             nc.sync.dma_start(w1_raw[e][:].bitcast(I32), w1_words[e, 0].bitcast(I32))
 
@@ -107,9 +109,9 @@ def tile_moe_pkd_mlp_silu_kernel(
             for i in range(count):
                 xsg[first + i] = scales[:, i * CHUNK : (i + 1) * CHUNK]
 
-        def permute_w1(e, s, raw):
+        def permute_w1(e, s, raw, copy=nc.vector.tensor_copy):
             w1p[(e, s)] = keep.tile([P, 2 * K_PASS], U8, name="w1p%d_%d" % (e, s), align_bytes=64)
-            nc.vector.tensor_copy(
+            copy(
                 out=w1p[(e, s)][:].bitcast(U16).rearrange("p (t m) -> p t m", t=PACK),
                 in_=raw.bitcast(U16).rearrange("p (m t) -> p t m", t=PACK),
             )
@@ -162,7 +164,7 @@ def tile_moe_pkd_mlp_silu_kernel(
             )
 
         banks = {}
-        sum_bank = {(0, 0): 0, (0, 4): 1, (1, 0): 2, (1, 4): 3, (0, 7): 4, (2, 0): 5, (2, 4): 6, (3, 0): 0, (3, 4): 7}
+        sum_bank = {(0, 0): 0, (1, 0): 1, (2, 0): 2, (0, 4): 3, (1, 4): 4, (0, 6): 5, (2, 4): 6, (3, 0): 5, (3, 4): 4}
 
         def second_layer(j, c, first, count=2):
             e = c * CHUNK // C
@@ -203,7 +205,7 @@ def tile_moe_pkd_mlp_silu_kernel(
         fetched = {}
 
         def fetch(j, blocks=4):
-            fetched[j] = turn.tile([P, T], F32, name="fetched%d" % j, offset=2 * H * (E - 1) + 4 * T * j, align_bytes=64)
+            fetched[j] = turn.tile([P, T], F32, name="fetched%d" % j, offset=2 * H * (E - 1) + 4 * T * (j % 2), align_bytes=64)
             nc.scalar.activation(
                 fetched[j][:, 0 : blocks * P], y[j][:].indirect(pos1_sb[:, 0 : blocks * P // GROUP]), COPY
             )
@@ -211,7 +213,7 @@ def tile_moe_pkd_mlp_silu_kernel(
         turned, scaled, back = {}, {}, {}
 
         def turn_over(j, blocks=4):
-            turned[j] = bank((1, 2, 4)[j], [P, T // P, P], "turned")
+            turned[j] = bank((7, 0, 1)[j], [P, T // P, P], "turned")
             for b in range(blocks):
                 nc.tensor.transpose(turned[j][:, b, :], fetched[j][:, b * P : (b + 1) * P], ident[:])
 
@@ -242,13 +244,13 @@ def tile_moe_pkd_mlp_silu_kernel(
         xsg_first = keep.tile([P, 3 * CHUNK], U8, name="xsg_first", align_bytes=64)
         gather_scales(0, 3, xsg_first[:])
         gather_words(0, 2, xg_first[:])
-        permute_w1(0, 0, w1_first[:])
+        permute_w1(0, 0, w1_zero[:, 0 : 2 * K_PASS], nc.scalar.copy)
+        permute_w1(0, 1, w1_zero[:, 2 * K_PASS : 4 * K_PASS], nc.scalar.copy)
         permute_w1_scales(0, 0, 2)
         permute_w1_scales(0, 2, 2)
         first_layer(0, 0)
         permute_w1_scales(1, 0, PACK)
         first_layer(1, 0)
-        permute_w1(0, 1, w1_second[:])
         first_layer(0, 1)
         first_layer(1, 1)
 
@@ -289,46 +291,42 @@ def tile_moe_pkd_mlp_silu_kernel(
             second_layer(0, 2 * e, 4 * (e // 2))
         quantize(3, 0)
         quantize(3, 1, slice(0, CHUNK))
-        second_layer(0, 6, 4, 1)
         quantize(3, 1, slice(CHUNK, C))
-        second_layer(0, 7, 7, 1)
+        second_layer(0, 6, 6)
         evacuate(0, 0, 4)
-        evacuate(0, 4, 7, nc.vector.tensor_copy)
-        evacuate(0, 7, 8)
+        evacuate(0, 4, 6, nc.vector.tensor_copy)
+        evacuate(0, 6, 8)
 
-        def sums(j):
+        for j in range(1, N_TILES):
             for first in (0, 4):
                 for c in (first, first + 2):
                     second_layer(j, c, first)
-
-        most = T - P
-        for j in range(1, N_TILES):
-            sums(j)
             evacuate(j, 0, 4, nc.vector.tensor_copy if j == 1 else nc.scalar.copy)
             evacuate(j, 4, 8)
         for j in range(N_TILES):
             pick(j, 1, 0, T)
+        most = T - P
         fetch(0)
         turn_over(0)
         fetch(1)
         turn_over(1)
         pick(3, 0, 0, T)
         weigh(0)
-        turn_back(0, 0, T, 3)
+        turn_back(0, 0, T, 2)
         fetch(2, 3)
         turn_over(2, 3)
         pick(2, 0, most, P)
         add(3, 0, T)
         store(3, 0, T)
         weigh(1)
-        turn_back(1, 0, T, 5)
+        turn_back(1, 0, T, 3)
         add(2, most, P)
         store(2, most, P)
         add(0, 0, T)
         store(0, 0, T)
         weigh(2, 3)
         turn_back(2, 0, 2 * P, 6)
-        turn_back(2, 2 * P, P, 7)
+        turn_back(2, 2 * P, P, 4)
         add(1, 0, T)
         store(1, 0, T)
         add(2, 0, 2 * P)

@@ -47,7 +47,15 @@ def tile_moe_pkd_mlp_silu_kernel(
         xs = keep.tile([P, T], U8, name="xs", align_bytes=64)
         ident = keep.tile([P, P], F32, name="ident")
         w1sp = [keep.tile([P, H], U8, name="w1sp%d" % e, align_bytes=64) for e in range(E)]
-        w2w = [keep.tile([P, H_PASSES, 2 * N], U8, name="w2w%d" % e, align_bytes=64) for e in range(E)]
+        w2w = {}
+        for pair in range(2):
+            for side in range(2):
+                if (pair, side) == (0, 0):
+                    w2w[(pair, side)] = turn.tile([P, 2 * H_PASSES, N], U8, name="w2w00", offset=12288, align_bytes=64)
+                else:
+                    w2w[(pair, side)] = keep.tile(
+                        [P, 2 * H_PASSES, N], U8, name="w2w%d%d" % (pair, side), align_bytes=64
+                    )
         w2s = keep.tile([P, E * H_PASSES, N], U8, name="w2s", align_bytes=64)
         gates = keep.tile([P, 2, T], F32, name="gates")
         gate_cols = keep.tile([P, T // P], F32, name="gate_cols")
@@ -158,7 +166,7 @@ def tile_moe_pkd_mlp_silu_kernel(
 
         def quantize(e, s, places=slice(0, C)):
             nc.vector.quantize_mx(
-                out=hq[:, e, s, places].bitcast(FP8X4),
+                out=hq[e][:, s, places].bitcast(FP8X4),
                 scales=hs[:, e, s, places],
                 in_=h_bf[(e, s)][:, places, :].rearrange("p c t -> p (c t)"),
             )
@@ -174,9 +182,9 @@ def tile_moe_pkd_mlp_silu_kernel(
             for s in range(H_PASSES):
                 nc.tensor.matmul_mx(
                     out=banks[(j, first)][:, (c - first) * CHUNK : (c - first + count) * CHUNK],
-                    lhsT=w2w[e][:, s, 2 * j * P : 2 * (j + 1) * P].bitcast(FP4X4),
+                    lhsT=w2w[(e // 2, j // 2)][:, (e % 2) * H_PASSES + s, 2 * (j % 2) * P : 2 * (j % 2 + 1) * P].bitcast(FP4X4),
                     lhsT_scale=w2s[:, e * H_PASSES + s, j * P : (j + 1) * P],
-                    rhs=hq[:, e, s, places].bitcast(FP8X4),
+                    rhs=hq[e][:, s, places].bitcast(FP8X4),
                     rhs_scale=hs[:, e, s, places],
                     start=(s == 0),
                     stop=(s == H_PASSES - 1),
@@ -260,8 +268,10 @@ def tile_moe_pkd_mlp_silu_kernel(
             shift_w1_scales(e)
         for r in range(4):
             nc.sync.dma_start(w2s[r:P:32, :, :].bitcast(I32), w2s_rows[r].bitcast(I32))
-        for e in range(E):
-            nc.sync.dma_start(w2w[e][:].bitcast(I32), w2_words[e].rearrange("s p b -> p s b").bitcast(I32))
+        for side in range(2):
+            for pair in range(2):
+                rows = w2_words[2 * pair : 2 * pair + 2, :, :, side * N : (side + 1) * N].rearrange("e s p b -> p (e s) b")
+                nc.sync.dma_start(w2w[(pair, side)][:].bitcast(I32), rows.bitcast(I32))
         nc.sync.dma_start(pos1_sb[:], pos1)
         nc.sync.dma_start(pos2_sb[:], pos2)
         nc.sync.dma_start(gates[:], gate[:, 0:P, :].rearrange("g p t -> p g t"))
@@ -284,24 +294,32 @@ def tile_moe_pkd_mlp_silu_kernel(
             first_layer(2 * e, 1)
             first_layer(2 * e + 1, 1)
 
-        hq = turn.tile([P, E, H_PASSES, C], U32, name="hq", offset=2 * H * (E - 1), align_bytes=64)
+        early = turn.tile([P, E - 1, H_PASSES, C], U32, name="early", offset=2 * H * (E - 1), align_bytes=64)
+        hq = [early[:, e, :, :] for e in range(E - 1)]
         for e in range(E - 1):
             quantize(e, 0)
             quantize(e, 1)
-            second_layer(0, 2 * e, 4 * (e // 2))
+        for j in range(2):
+            second_layer(j, 0, 0)
+            second_layer(j, 2, 0)
+            evacuate(j, 0, 4, nc.vector.tensor_copy)
+        second_layer(0, 4, 4)
+        late = turn.tile([P, H_PASSES, C], U32, name="late", offset=12288, align_bytes=64)
+        hq.append(late[:])
         quantize(3, 0)
         quantize(3, 1, slice(0, CHUNK))
         quantize(3, 1, slice(CHUNK, C))
         second_layer(0, 6, 6)
-        evacuate(0, 0, 4)
         evacuate(0, 4, 6, nc.vector.tensor_copy)
         evacuate(0, 6, 8)
-
-        for j in range(1, N_TILES):
+        second_layer(1, 4, 4)
+        second_layer(1, 6, 4)
+        evacuate(1, 4, 8)
+        for j in range(2, N_TILES):
             for first in (0, 4):
                 for c in (first, first + 2):
                     second_layer(j, c, first)
-            evacuate(j, 0, 4, nc.vector.tensor_copy if j == 1 else nc.scalar.copy)
+            evacuate(j, 0, 4)
             evacuate(j, 4, 8)
         for j in range(N_TILES):
             pick(j, 1, 0, T)

@@ -11,8 +11,21 @@ K_PASS = P * PACK
 H_PASSES = H // K_PASS
 N_TILES = N // P
 CHUNK = 128
-CHUNKS = SLOTS // CHUNK
 GROUP = 16
+QUADRANT = 32
+ROWS = 4
+BANKS = 8
+BLOCKS = T // P
+
+SCALAR_BLOCKS = (0, 4, 4, 3)
+
+RAW_BYTES = 2 * H
+CODES_AT = RAW_BYTES * (E - 1)
+LATE_AT = CODES_AT + 4 * (E - 1) * H_PASSES * C
+
+SUM_BANK = {(0, 0): 0, (1, 0): 1, (2, 0): 2, (0, 4): 3, (1, 4): 4, (0, 7): 5, (2, 4): 6, (3, 0): 5, (3, 4): 4}
+TURN_BANK = {1: 7, 2: 0, 3: 1}
+BACK_BANK = {(1, 0): 2, (2, 0): 3, (3, 0): 6, (3, 2 * P): 4}
 
 F32 = mybir.dt.float32
 BF16 = mybir.dt.bfloat16
@@ -36,7 +49,7 @@ def tile_moe_pkd_mlp_silu_kernel(
     nc = tc.nc
     with ExitStack() as ctx:
         keep = ctx.enter_context(tc.tile_pool(name="keep", bufs=1))
-        ring = ctx.enter_context(tc.tile_pool(name="ring", bufs=4))
+        ring = ctx.enter_context(tc.tile_pool(name="ring", bufs=N_TILES))
         turn = ctx.enter_context(tc.tile_pool(name="turn", bufs=1))
         psum = ctx.enter_context(tc.psum_pool(name="psum", bufs=1))
 
@@ -46,63 +59,54 @@ def tile_moe_pkd_mlp_silu_kernel(
         xw = keep.tile([P, T], I32, name="xw", align_bytes=64)
         xs = keep.tile([P, T], U8, name="xs", align_bytes=64)
         ident = keep.tile([P, P], F32, name="ident")
-        w1sp = [keep.tile([P, H], U8, name="w1sp%d" % e, align_bytes=64) for e in range(E)]
-        w2w = {}
-        for pair in range(2):
-            for side in range(2):
-                if (pair, side) == (0, 0):
-                    w2w[(pair, side)] = turn.tile([P, 2 * H_PASSES, N], U8, name="w2w00", offset=12288, align_bytes=64)
-                else:
-                    w2w[(pair, side)] = keep.tile(
-                        [P, 2 * H_PASSES, N], U8, name="w2w%d%d" % (pair, side), align_bytes=64
-                    )
-        w2s = keep.tile([P, E * H_PASSES, N], U8, name="w2s", align_bytes=64)
+        w1_plane = [keep.tile([P, H], U8, name="w1_plane%d" % e, align_bytes=64) for e in range(E)]
+        w2w = {(0, 0): turn.tile([P, 2 * H_PASSES, N], U8, name="w2w00", offset=LATE_AT, align_bytes=64)}
+        for pair, side in ((0, 1), (1, 0), (1, 1)):
+            w2w[(pair, side)] = keep.tile([P, 2 * H_PASSES, N], U8, name="w2w%d%d" % (pair, side), align_bytes=64)
+        w2_plane = keep.tile([P, E * H_PASSES, N], U8, name="w2_plane", align_bytes=64)
         gates = keep.tile([P, 2, T], F32, name="gates")
-        gate_cols = keep.tile([P, T // P], F32, name="gate_cols")
-        hs = keep.tile([P, E, H_PASSES, C], U8, name="hs", align_bytes=64)
+        gate_cols = keep.tile([P, BLOCKS], F32, name="gate_cols")
+        h_plane = keep.tile([P, E, H_PASSES, C], U8, name="h_plane", align_bytes=64)
         y = [keep.tile([P, SLOTS], F32, name="y%d" % j) for j in range(N_TILES)]
 
-        w1_zero = keep.tile([P, 2 * H], U8, name="w1_zero", align_bytes=64)
-        held = turn.tile([P, H], U8, name="held", offset=0, align_bytes=64)
+        w1_raw = {0: keep.tile([P, RAW_BYTES], U8, name="w1_raw0", align_bytes=64)}
+        w1s_raw = turn.tile([P, H], U8, name="w1s_raw", offset=0, align_bytes=64)
         warm = keep.tile([P, 2], F32, name="warm")
-        w1_raw = {}
         for e in range(1, E):
-            w1_raw[e] = turn.tile([P, 2 * H], U8, name="w1_raw%d" % e, offset=2 * H * e, align_bytes=64)
+            w1_raw[e] = turn.tile([P, RAW_BYTES], U8, name="w1_raw%d" % e, offset=RAW_BYTES * e, align_bytes=64)
 
-        w1s_raw = held
         nc.gpsimd.memset(w1s_raw[:].bitcast(I32), 0)
         nc.vector.memset(warm[:, 0:1], 0.0)
         for e in range(1, E):
-            nc.vector.memset(w1sp[e][96:P, :].bitcast(I32), 0)
-        nc.vector.memset(w2s[:].rearrange("p a n -> p (a n)").bitcast(I32), 0)
+            nc.vector.memset(w1_plane[e][3 * QUADRANT : P, :].bitcast(I32), 0)
+        nc.vector.memset(w2_plane[:].rearrange("p a n -> p (a n)").bitcast(I32), 0)
         make_identity(nc, ident[:])
 
-        w2s_rows = w2_scales.rearrange("e s (q r) n -> r q (e s) n", r=4)
-
         def load_x_scales(queue, q):
-            rows = x_scales[0, 4 * q : 4 * q + 4, :].bitcast(I32)
-            queue.dma_start(xs[32 * q : 32 * q + 32, :].bitcast(I32), rows.unsqueeze(0).to_broadcast([8, 4, T // 4]))
+            rows = x_scales[0, ROWS * q : ROWS * (q + 1), :].bitcast(I32)
+            queue.dma_start(
+                xs[QUADRANT * q : QUADRANT * (q + 1), :].bitcast(I32),
+                rows.unsqueeze(0).to_broadcast([QUADRANT // ROWS, ROWS, T // 4]),
+            )
 
         def load_w1_scales(queue, q):
             queue.dma_start(
-                w1s_raw[32 * q : 32 * q + 4 * E, :].bitcast(I32), w1_scales[:, 0, 4 * q : 4 * q + 4, :].bitcast(I32)
+                w1s_raw[QUADRANT * q : QUADRANT * q + ROWS * E, :].bitcast(I32),
+                w1_scales[:, 0, ROWS * q : ROWS * (q + 1), :].bitcast(I32),
             )
 
         nc.sync.dma_start(offs_sb[:], offs)
-        load_x_scales(nc.scalar, 0)
-        load_x_scales(nc.sync, 1)
-        load_x_scales(nc.scalar, 2)
-        load_x_scales(nc.sync, 3)
-        nc.scalar.dma_start(w1_zero[:].bitcast(I32), w1_words[0, 0].bitcast(I32))
+        for q in range(P // QUADRANT):
+            load_x_scales(nc.sync if q % 2 else nc.scalar, q)
+        nc.scalar.dma_start(w1_raw[0][:].bitcast(I32), w1_words[0, 0].bitcast(I32))
         nc.sync.dma_start(xw[:], x_words[0].rearrange("p t r -> p (t r)").bitcast(I32))
-        load_w1_scales(nc.scalar, 0)
-        for q in range(1, 4):
-            load_w1_scales(nc.sync, q)
+        for q in range(P // QUADRANT):
+            load_w1_scales(nc.sync if q else nc.scalar, q)
         nc.scalar.activation(out=warm[:, 1:2], in_=warm[:, 0:1], func=SILU)
         for e in range(1, E):
             nc.sync.dma_start(w1_raw[e][:].bitcast(I32), w1_words[e, 0].bitcast(I32))
 
-        xg, xsg, w1p = {}, {}, {}
+        xg, xsg, w1w = {}, {}, {}
 
         def entries(first, count):
             return offs_sb[:, first * CHUNK // GROUP : (first + count) * CHUNK // GROUP]
@@ -117,25 +121,26 @@ def tile_moe_pkd_mlp_silu_kernel(
             for i in range(count):
                 xsg[first + i] = scales[:, i * CHUNK : (i + 1) * CHUNK]
 
-        def permute_w1(e, s, raw, copy=nc.vector.tensor_copy):
-            w1p[(e, s)] = keep.tile([P, 2 * K_PASS], U8, name="w1p%d_%d" % (e, s), align_bytes=64)
+        def reorder_words(e, s, copy):
+            w1w[(e, s)] = keep.tile([P, 2 * K_PASS], U8, name="w1w%d_%d" % (e, s), align_bytes=64)
+            raw = w1_raw[e][:, 2 * K_PASS * s : 2 * K_PASS * (s + 1)]
             copy(
-                out=w1p[(e, s)][:].bitcast(U16).rearrange("p (t m) -> p t m", t=PACK),
+                out=w1w[(e, s)][:].bitcast(U16).rearrange("p (t m) -> p t m", t=PACK),
                 in_=raw.bitcast(U16).rearrange("p (m t) -> p t m", t=PACK),
             )
 
-        def permute_w1_scales(s, first, count):
+        def reorder_scales(s, first, count):
             cols = slice(s * K_PASS, (s + 1) * K_PASS)
             nc.vector.tensor_copy(
-                out=w1sp[0][:, cols].rearrange("p (t m) -> p t m", t=PACK)[:, first : first + count, :],
+                out=w1_plane[0][:, cols].rearrange("p (t m) -> p t m", t=PACK)[:, first : first + count, :],
                 in_=w1s_raw[:, cols].rearrange("p (m t) -> p t m", t=PACK)[:, first : first + count, :],
             )
 
-        def shift_w1_scales(e, cols=slice(0, H)):
-            for first, count in ((0, 64), (64, 32), (96, 4)):
+        def move_plane(e, cols):
+            for first, count in ((0, 2 * QUADRANT), (2 * QUADRANT, QUADRANT), (3 * QUADRANT, ROWS)):
                 nc.sync.dma_start(
-                    w1sp[e][first : first + count, cols].bitcast(I32),
-                    w1sp[0][first + 4 * e : first + 4 * e + count, cols].bitcast(I32),
+                    w1_plane[e][first : first + count, cols].bitcast(I32),
+                    w1_plane[0][first + ROWS * e : first + ROWS * e + count, cols].bitcast(I32),
                 )
 
         def bank(b, shape, name):
@@ -149,54 +154,55 @@ def tile_moe_pkd_mlp_silu_kernel(
             if (e, s) not in h_bf:
                 h_bf[(e, s)] = keep.tile([P, C, PACK], BF16, name="h_bf%d_%d" % (e, s), align_bytes=64)
             place = c * CHUNK - e * C
-            a = bank(len(groups) % 8, [P, PACK, CHUNK], "a")
+            a = bank(len(groups) % BANKS, [P, PACK, CHUNK], "a")
             groups.append(a)
             for t in range(PACK):
                 col = s * K_PASS + t * P
                 nc.tensor.matmul_mx(
                     out=a[:, t, :],
-                    lhsT=w1p[(e, s)][:, 2 * t * P : 2 * (t + 1) * P].bitcast(FP4X4),
-                    lhsT_scale=w1sp[e][:, col : col + P],
+                    lhsT=w1w[(e, s)][:, 2 * t * P : 2 * (t + 1) * P].bitcast(FP4X4),
+                    lhsT_scale=w1_plane[e][:, col : col + P],
                     rhs=xg[c].bitcast(FP8X4),
                     rhs_scale=xsg[c],
                     start=True,
                     stop=True,
                 )
-            nc.scalar.activation(out=h_bf[(e, s)][:, place : place + CHUNK, :], in_=a[:].rearrange("p t c -> p c t"), func=SILU)
+            nc.scalar.activation(
+                out=h_bf[(e, s)][:, place : place + CHUNK, :], in_=a[:].rearrange("p t c -> p c t"), func=SILU
+            )
 
-        def quantize(e, s, places=slice(0, C)):
+        h_codes = []
+
+        def quantize(e, s, places):
             nc.vector.quantize_mx(
-                out=hq[e][:, s, places].bitcast(FP8X4),
-                scales=hs[:, e, s, places],
+                out=h_codes[e][:, s, places].bitcast(FP8X4),
+                scales=h_plane[:, e, s, places],
                 in_=h_bf[(e, s)][:, places, :].rearrange("p c t -> p (c t)"),
             )
 
-        banks = {}
-        sum_bank = {(0, 0): 0, (1, 0): 1, (2, 0): 2, (0, 4): 3, (1, 4): 4, (0, 6): 5, (2, 4): 6, (3, 0): 5, (3, 4): 4}
+        sums = {}
 
         def second_layer(j, c, first, count=2):
             e = c * CHUNK // C
             places = slice(c * CHUNK - e * C, (c + count) * CHUNK - e * C)
-            if (j, first) not in banks:
-                banks[(j, first)] = bank(sum_bank[(j, first)], [P, 4 * CHUNK], "yb")
+            if (j, first) not in sums:
+                sums[(j, first)] = bank(SUM_BANK[(j, first)], [P, 4 * CHUNK], "sums")
+            words = w2w[(e // 2, j // 2)]
             for s in range(H_PASSES):
                 nc.tensor.matmul_mx(
-                    out=banks[(j, first)][:, (c - first) * CHUNK : (c - first + count) * CHUNK],
-                    lhsT=w2w[(e // 2, j // 2)][:, (e % 2) * H_PASSES + s, 2 * (j % 2) * P : 2 * (j % 2 + 1) * P].bitcast(FP4X4),
-                    lhsT_scale=w2s[:, e * H_PASSES + s, j * P : (j + 1) * P],
-                    rhs=hq[e][:, s, places].bitcast(FP8X4),
-                    rhs_scale=hs[:, e, s, places],
+                    out=sums[(j, first)][:, (c - first) * CHUNK : (c - first + count) * CHUNK],
+                    lhsT=words[:, (e % 2) * H_PASSES + s, 2 * (j % 2) * P : 2 * (j % 2 + 1) * P].bitcast(FP4X4),
+                    lhsT_scale=w2_plane[:, e * H_PASSES + s, j * P : (j + 1) * P],
+                    rhs=h_codes[e][:, s, places].bitcast(FP8X4),
+                    rhs_scale=h_plane[:, e, s, places],
                     start=(s == 0),
                     stop=(s == H_PASSES - 1),
                 )
 
-        def evacuate(j, first, last, copy=nc.scalar.copy):
-            copy(
-                out=y[j][:, first * CHUNK : last * CHUNK],
-                in_=banks[(j, first)][:, 0 : (last - first) * CHUNK],
-            )
+        def evacuate(j, first, last, copy):
+            copy(out=y[j][:, first * CHUNK : last * CHUNK], in_=sums[(j, first)][:, 0 : (last - first) * CHUNK])
 
-        picked = {}
+        picked, fetched, turned, scaled, back, results = {}, {}, {}, {}, {}, {}
 
         def pick(j, g, first, count):
             tokens = slice(first, first + count)
@@ -210,68 +216,61 @@ def tile_moe_pkd_mlp_silu_kernel(
                 MULT,
             )
 
-        fetched = {}
-
-        def fetch(j, blocks=4):
-            fetched[j] = turn.tile([P, T], F32, name="fetched%d" % j, offset=2 * H * (E - 1) + 4 * T * (j % 2), align_bytes=64)
+        def fetch(j):
+            blocks = SCALAR_BLOCKS[j]
+            fetched[j] = turn.tile(
+                [P, T], F32, name="fetched%d" % j, offset=CODES_AT + 4 * T * (j % 2), align_bytes=64
+            )
             nc.scalar.activation(
                 fetched[j][:, 0 : blocks * P], y[j][:].indirect(pos1_sb[:, 0 : blocks * P // GROUP]), COPY
             )
-
-        turned, scaled, back = {}, {}, {}
-
-        def turn_over(j, blocks=4):
-            turned[j] = bank((7, 0, 1)[j], [P, T // P, P], "turned")
+            turned[j] = bank(TURN_BANK[j], [P, BLOCKS, P], "turned")
             for b in range(blocks):
                 nc.tensor.transpose(turned[j][:, b, :], fetched[j][:, b * P : (b + 1) * P], ident[:])
 
-        def weigh(j, blocks=4):
-            scaled[j] = ring.tile([P, T // P, P], F32, name="scaled")
-            for b in range(blocks):
+        def weigh(j):
+            scaled[j] = ring.tile([P, BLOCKS, P], F32, name="scaled")
+            for b in range(SCALAR_BLOCKS[j]):
                 nc.scalar.activation(scaled[j][:, b, :], turned[j][:, b, :], COPY, scale=gate_cols[:, b : b + 1])
 
-        def turn_back(j, first, count, b0):
-            back[(j, first)] = bank(b0, [P, T], "back")
+        def turn_back(j, first, count):
+            back[(j, first)] = bank(BACK_BANK[(j, first)], [P, T], "back")
             for b in range(first // P, (first + count) // P):
                 nc.tensor.transpose(back[(j, first)][:, b * P : (b + 1) * P], scaled[j][:, b, :], ident[:])
 
-        results = {}
-
-        def add(j, first, count):
+        def finish(j, first, count):
             tokens = slice(first, first + count)
             if j not in results:
                 results[j] = ring.tile([P, T], F32, name="result")
             weighted = back[(j, first)][:, tokens] if (j, first) in back else picked[j][:, 0, tokens]
             nc.vector.tensor_tensor(results[j][:, tokens], weighted, picked[j][:, 1, tokens], ADD)
-
-        def store(j, first, count):
-            tokens = slice(first, first + count)
             nc.sync.dma_start(out[j * P : (j + 1) * P, tokens], results[j][:, tokens])
 
         xg_first = keep.tile([P, C], U32, name="xg_first", align_bytes=64)
         xsg_first = keep.tile([P, 3 * CHUNK], U8, name="xsg_first", align_bytes=64)
         gather_scales(0, 3, xsg_first[:])
         gather_words(0, 2, xg_first[:])
-        permute_w1(0, 0, w1_zero[:, 0 : 2 * K_PASS], nc.scalar.copy)
-        permute_w1(0, 1, w1_zero[:, 2 * K_PASS : 4 * K_PASS], nc.scalar.copy)
-        permute_w1_scales(0, 0, 2)
-        permute_w1_scales(0, 2, 2)
+        for s in range(H_PASSES):
+            reorder_words(0, s, nc.scalar.copy)
+        reorder_scales(0, 0, PACK // 2)
+        reorder_scales(0, PACK // 2, PACK // 2)
         first_layer(0, 0)
-        permute_w1_scales(1, 0, PACK)
+        reorder_scales(1, 0, PACK)
         first_layer(1, 0)
         first_layer(0, 1)
         first_layer(1, 1)
 
         for s in range(H_PASSES):
-            shift_w1_scales(1, slice(s * K_PASS, (s + 1) * K_PASS))
+            move_plane(1, slice(s * K_PASS, (s + 1) * K_PASS))
         for e in range(2, E):
-            shift_w1_scales(e)
-        for r in range(4):
-            nc.sync.dma_start(w2s[r:P:32, :, :].bitcast(I32), w2s_rows[r].bitcast(I32))
+            move_plane(e, slice(0, H))
+        w2s_rows = w2_scales.rearrange("e s (q r) n -> r q (e s) n", r=ROWS)
+        for r in range(ROWS):
+            nc.sync.dma_start(w2_plane[r:P:QUADRANT, :, :].bitcast(I32), w2s_rows[r].bitcast(I32))
         for side in range(2):
             for pair in range(2):
-                rows = w2_words[2 * pair : 2 * pair + 2, :, :, side * N : (side + 1) * N].rearrange("e s p b -> p (e s) b")
-                nc.sync.dma_start(w2w[(pair, side)][:].bitcast(I32), rows.bitcast(I32))
+                rows = w2_words[2 * pair : 2 * pair + 2, :, :, side * N : (side + 1) * N]
+                nc.sync.dma_start(w2w[(pair, side)][:].bitcast(I32), rows.rearrange("e s p b -> p (e s) b").bitcast(I32))
         nc.sync.dma_start(pos1_sb[:], pos1)
         nc.sync.dma_start(pos2_sb[:], pos2)
         nc.sync.dma_start(gates[:], gate[:, 0:P, :].rearrange("g p t -> p g t"))
@@ -279,75 +278,68 @@ def tile_moe_pkd_mlp_silu_kernel(
             nc.sync.dma_start(gate_cols[:], gate[0, 0, :].rearrange("(b p) -> p b", p=P))
 
         for e in range(1, E):
-            base = 2 * H * (e - 1)
+            base = RAW_BYTES * (e - 1)
             scales = turn.tile([P, C], U8, name="xsg%d" % e, offset=base, align_bytes=64)
             words = turn.tile([P, C], U32, name="xg%d" % e, offset=base + C, align_bytes=64)
-            permute_w1(e, 0, w1_raw[e][:, 0 : 2 * K_PASS])
+            missing = [c for c in (2 * e, 2 * e + 1) if c not in xsg]
+            reorder_words(e, 0, nc.vector.tensor_copy)
             gather_words(2 * e, 2, words[:])
-            if e == 1:
-                gather_scales(3, 1, scales[:, 0:CHUNK])
-            else:
-                gather_scales(2 * e, 2, scales[:])
+            gather_scales(missing[0], len(missing), scales[:, 0 : len(missing) * CHUNK])
             first_layer(2 * e, 0)
             first_layer(2 * e + 1, 0)
-            permute_w1(e, 1, w1_raw[e][:, 2 * K_PASS : 4 * K_PASS])
+            reorder_words(e, 1, nc.vector.tensor_copy)
             first_layer(2 * e, 1)
             first_layer(2 * e + 1, 1)
 
-        early = turn.tile([P, E - 1, H_PASSES, C], U32, name="early", offset=2 * H * (E - 1), align_bytes=64)
-        hq = [early[:, e, :, :] for e in range(E - 1)]
+        early = turn.tile([P, E - 1, H_PASSES, C], U32, name="early", offset=CODES_AT, align_bytes=64)
         for e in range(E - 1):
-            quantize(e, 0)
-            quantize(e, 1)
+            h_codes.append(early[:, e, :, :])
+            for s in range(H_PASSES):
+                quantize(e, s, slice(0, C))
         for j in range(2):
             second_layer(j, 0, 0)
             second_layer(j, 2, 0)
             evacuate(j, 0, 4, nc.vector.tensor_copy)
         second_layer(0, 4, 4)
-        late = turn.tile([P, H_PASSES, C], U32, name="late", offset=12288, align_bytes=64)
-        hq.append(late[:])
-        quantize(3, 0)
-        quantize(3, 1, slice(0, CHUNK))
-        quantize(3, 1, slice(CHUNK, C))
-        second_layer(0, 6, 6)
-        evacuate(0, 4, 6, nc.vector.tensor_copy)
-        evacuate(0, 6, 8)
+        late = turn.tile([P, H_PASSES, C], U32, name="late", offset=LATE_AT, align_bytes=64)
+        h_codes.append(late[:])
+        quantize(E - 1, 0, slice(0, C))
+        quantize(E - 1, 1, slice(0, CHUNK))
+        quantize(E - 1, 1, slice(CHUNK, C))
+        second_layer(0, 7, 7, 1)
+        second_layer(0, 6, 4, 1)
+        evacuate(0, 7, 8, nc.scalar.copy)
+        evacuate(0, 4, 7, nc.vector.tensor_copy)
         second_layer(1, 4, 4)
         second_layer(1, 6, 4)
-        evacuate(1, 4, 8)
+        evacuate(1, 4, 8, nc.scalar.copy)
         for j in range(2, N_TILES):
             for first in (0, 4):
-                for c in (first, first + 2):
-                    second_layer(j, c, first)
-            evacuate(j, 0, 4)
-            evacuate(j, 4, 8)
-        for j in range(N_TILES):
-            pick(j, 1, 0, T)
-        most = T - P
-        fetch(0)
-        turn_over(0)
+                second_layer(j, first, first)
+                second_layer(j, first + 2, first)
+            for first in (0, 4):
+                evacuate(j, first, first + 4, nc.scalar.copy)
+
+        split = SCALAR_BLOCKS[3] * P
+        pick(0, 1, 0, T)
+        pick(0, 0, 0, T)
+        pick(1, 1, 0, T)
+        finish(0, 0, T)
+        pick(2, 1, 0, T)
+        pick(3, 1, 0, T)
         fetch(1)
-        turn_over(1)
-        pick(3, 0, 0, T)
-        weigh(0)
-        turn_back(0, 0, T, 2)
-        fetch(2, 3)
-        turn_over(2, 3)
-        pick(2, 0, most, P)
-        add(3, 0, T)
-        store(3, 0, T)
+        fetch(2)
         weigh(1)
-        turn_back(1, 0, T, 3)
-        add(2, most, P)
-        store(2, most, P)
-        add(0, 0, T)
-        store(0, 0, T)
-        weigh(2, 3)
-        turn_back(2, 0, 2 * P, 6)
-        turn_back(2, 2 * P, P, 4)
-        add(1, 0, T)
-        store(1, 0, T)
-        add(2, 0, 2 * P)
-        store(2, 0, 2 * P)
-        add(2, 2 * P, P)
-        store(2, 2 * P, P)
+        turn_back(1, 0, T)
+        fetch(3)
+        pick(3, 0, split, T - split)
+        weigh(2)
+        turn_back(2, 0, T)
+        finish(1, 0, T)
+        finish(3, split, T - split)
+        weigh(3)
+        turn_back(3, 0, 2 * P)
+        turn_back(3, 2 * P, P)
+        finish(2, 0, T)
+        finish(3, 0, 2 * P)
+        finish(3, 2 * P, P)

@@ -17,15 +17,17 @@ ROWS = 4
 BANKS = 8
 BLOCKS = T // P
 
-SCALAR_BLOCKS = (0, 4, 4, 3)
+SCALAR_BLOCKS = (0, 4, 3, 4)
 
 RAW_BYTES = 2 * H
 CODES_AT = RAW_BYTES * (E - 1)
 LATE_AT = CODES_AT + 4 * (E - 1) * H_PASSES * C
 
+SCALED_AT = LATE_AT + RAW_BYTES
+
 SUM_BANK = {(0, 0): 0, (1, 0): 1, (2, 0): 2, (0, 4): 3, (1, 4): 4, (0, 7): 5, (2, 4): 6, (3, 0): 5, (3, 4): 4}
-TURN_BANK = {1: 7, 2: 0, 3: 1}
-BACK_BANK = {(1, 0): 2, (2, 0): 3, (3, 0): 6, (3, 2 * P): 4}
+TURN_BANK = {(1, 0): 7, (2, 0): 0, (3, 0): 1, (3, 2): 5}
+BACK_BANK = {(1, 0): 2, (2, 0): 3, (3, 0): 6, (3, 2 * P): 4, (3, 3 * P): 7}
 
 F32 = mybir.dt.float32
 BF16 = mybir.dt.bfloat16
@@ -202,7 +204,7 @@ def tile_moe_pkd_mlp_silu_kernel(
         def evacuate(j, first, last, copy):
             copy(out=y[j][:, first * CHUNK : last * CHUNK], in_=sums[(j, first)][:, 0 : (last - first) * CHUNK])
 
-        picked, fetched, turned, scaled, back, results = {}, {}, {}, {}, {}, {}
+        picked, turned, scaled, back, results = {}, {}, {}, {}, {}
 
         def pick(j, g, first, count):
             tokens = slice(first, first + count)
@@ -216,27 +218,25 @@ def tile_moe_pkd_mlp_silu_kernel(
                 MULT,
             )
 
-        def fetch(j):
-            blocks = SCALAR_BLOCKS[j]
-            fetched[j] = turn.tile(
-                [P, T], F32, name="fetched%d" % j, offset=CODES_AT + 4 * T * (j % 2), align_bytes=64
-            )
-            nc.scalar.activation(
-                fetched[j][:, 0 : blocks * P], y[j][:].indirect(pos1_sb[:, 0 : blocks * P // GROUP]), COPY
-            )
-            turned[j] = bank(TURN_BANK[j], [P, BLOCKS, P], "turned")
+        def fetch(j, first, blocks, at):
+            values = turn.tile([P, blocks * P], F32, name="fetched%d_%d" % (j, first), offset=at, align_bytes=64)
+            pos = pos1_sb[:, first * P // GROUP : (first + blocks) * P // GROUP]
+            nc.scalar.activation(values[:], y[j][:].indirect(pos), COPY)
+            into = bank(TURN_BANK[(j, first)], [P, BLOCKS, P], "turned")
             for b in range(blocks):
-                nc.tensor.transpose(turned[j][:, b, :], fetched[j][:, b * P : (b + 1) * P], ident[:])
+                turned[(j, first + b)] = into[:, b, :]
+                nc.tensor.transpose(into[:, b, :], values[:, b * P : (b + 1) * P], ident[:])
 
         def weigh(j):
-            scaled[j] = ring.tile([P, BLOCKS, P], F32, name="scaled")
             for b in range(SCALAR_BLOCKS[j]):
-                nc.scalar.activation(scaled[j][:, b, :], turned[j][:, b, :], COPY, scale=gate_cols[:, b : b + 1])
+                at = SCALED_AT + 4 * (T * (j - 1) + P * b)
+                scaled[(j, b)] = turn.tile([P, P], F32, name="scaled%d_%d" % (j, b), offset=at, align_bytes=64)
+                nc.scalar.activation(scaled[(j, b)][:], turned[(j, b)], COPY, scale=gate_cols[:, b : b + 1])
 
         def turn_back(j, first, count):
             back[(j, first)] = bank(BACK_BANK[(j, first)], [P, T], "back")
             for b in range(first // P, (first + count) // P):
-                nc.tensor.transpose(back[(j, first)][:, b * P : (b + 1) * P], scaled[j][:, b, :], ident[:])
+                nc.tensor.transpose(back[(j, first)][:, b * P : (b + 1) * P], scaled[(j, b)][:], ident[:])
 
         def finish(j, first, count):
             tokens = slice(first, first + count)
@@ -320,26 +320,29 @@ def tile_moe_pkd_mlp_silu_kernel(
             for first in (0, 4):
                 evacuate(j, first, first + 4, nc.scalar.copy)
 
-        split = SCALAR_BLOCKS[3] * P
+        split = SCALAR_BLOCKS[2] * P
         pick(0, 1, 0, T)
         pick(0, 0, 0, T)
         pick(1, 1, 0, T)
         finish(0, 0, T)
         pick(2, 1, 0, T)
         pick(3, 1, 0, T)
-        fetch(1)
-        fetch(2)
+        fetch(1, 0, BLOCKS, CODES_AT + 4 * T)
+        fetch(2, 0, SCALAR_BLOCKS[2], CODES_AT)
+        fetch(3, 0, 2, LATE_AT)
         weigh(1)
         turn_back(1, 0, T)
-        fetch(3)
-        pick(3, 0, split, T - split)
+        pick(2, 0, split, T - split)
         weigh(2)
-        turn_back(2, 0, T)
+        turn_back(2, 0, split)
+        fetch(3, 2, 2, SCALED_AT)
         finish(1, 0, T)
-        finish(3, split, T - split)
+        finish(2, split, T - split)
         weigh(3)
         turn_back(3, 0, 2 * P)
         turn_back(3, 2 * P, P)
-        finish(2, 0, T)
+        turn_back(3, 3 * P, P)
+        finish(2, 0, split)
         finish(3, 0, 2 * P)
         finish(3, 2 * P, P)
+        finish(3, 3 * P, P)

@@ -1,7 +1,6 @@
 from contextlib import ExitStack
 
 import concourse.mybir as mybir
-from concourse.masks import make_identity
 
 K, T, E, C, H, N = 512, 512, 4, 256, 1024, 512
 SLOTS = E * C
@@ -15,19 +14,12 @@ GROUP = 16
 QUADRANT = 32
 ROWS = 4
 BANKS = 8
-BLOCKS = T // P
-
-SCALAR_BLOCKS = (0, 4, 3, 4)
 
 RAW_BYTES = 2 * H
 CODES_AT = RAW_BYTES * (E - 1)
 LATE_AT = CODES_AT + 4 * (E - 1) * H_PASSES * C
 
-SCALED_AT = LATE_AT + RAW_BYTES
-
 SUM_BANK = {(0, 0): 0, (1, 0): 1, (2, 0): 2, (0, 4): 3, (1, 4): 4, (0, 7): 5, (2, 4): 6, (3, 0): 5, (3, 4): 4}
-TURN_BANK = {(1, 0): 7, (2, 0): 0, (3, 0): 1, (3, 2): 5}
-BACK_BANK = {(1, 0): 2, (2, 0): 3, (3, 0): 6, (3, 2 * P): 4, (3, 3 * P): 7}
 
 F32 = mybir.dt.float32
 BF16 = mybir.dt.bfloat16
@@ -51,7 +43,6 @@ def tile_moe_pkd_mlp_silu_kernel(
     nc = tc.nc
     with ExitStack() as ctx:
         keep = ctx.enter_context(tc.tile_pool(name="keep", bufs=1))
-        ring = ctx.enter_context(tc.tile_pool(name="ring", bufs=N_TILES))
         turn = ctx.enter_context(tc.tile_pool(name="turn", bufs=1))
         psum = ctx.enter_context(tc.psum_pool(name="psum", bufs=1))
 
@@ -60,14 +51,12 @@ def tile_moe_pkd_mlp_silu_kernel(
         pos2_sb = keep.tile([P, T // GROUP], U16, name="pos2_sb")
         xw = keep.tile([P, T], I32, name="xw", align_bytes=64)
         xs = keep.tile([P, T], U8, name="xs", align_bytes=64)
-        ident = keep.tile([P, P], F32, name="ident")
         w1_plane = [keep.tile([P, H], U8, name="w1_plane%d" % e, align_bytes=64) for e in range(E)]
         w2w = {(0, 0): turn.tile([P, 2 * H_PASSES, N], U8, name="w2w00", offset=LATE_AT, align_bytes=64)}
         for pair, side in ((0, 1), (1, 0), (1, 1)):
             w2w[(pair, side)] = keep.tile([P, 2 * H_PASSES, N], U8, name="w2w%d%d" % (pair, side), align_bytes=64)
         w2_plane = keep.tile([P, E * H_PASSES, N], U8, name="w2_plane", align_bytes=64)
         gates = keep.tile([P, 2, T], F32, name="gates")
-        gate_cols = keep.tile([P, BLOCKS], F32, name="gate_cols")
         h_plane = keep.tile([P, E, H_PASSES, C], U8, name="h_plane", align_bytes=64)
         y = [keep.tile([P, SLOTS], F32, name="y%d" % j) for j in range(N_TILES)]
 
@@ -82,7 +71,6 @@ def tile_moe_pkd_mlp_silu_kernel(
         for e in range(1, E):
             nc.vector.memset(w1_plane[e][3 * QUADRANT : P, :].bitcast(I32), 0)
         nc.vector.memset(w2_plane[:].rearrange("p a n -> p (a n)").bitcast(I32), 0)
-        make_identity(nc, ident[:])
 
         def load_x_scales(queue, q):
             rows = x_scales[0, ROWS * q : ROWS * (q + 1), :].bitcast(I32)
@@ -204,46 +192,27 @@ def tile_moe_pkd_mlp_silu_kernel(
         def evacuate(j, first, last, copy):
             copy(out=y[j][:, first * CHUNK : last * CHUNK], in_=sums[(j, first)][:, 0 : (last - first) * CHUNK])
 
-        picked, turned, scaled, back, results = {}, {}, {}, {}, {}
+        picked = [keep.tile([P, 2, T], F32, name="picked%d" % j) for j in range(N_TILES)]
+        results = [keep.tile([P, T], F32, name="result%d" % j) for j in range(N_TILES)]
+        fetched = {}
 
-        def pick(j, g, first, count):
-            tokens = slice(first, first + count)
-            pos = (pos1_sb, pos2_sb)[g]
-            if j not in picked:
-                picked[j] = ring.tile([P, 2, T], F32, name="picked")
-            nc.vector.tensor_tensor(
-                picked[j][:, g, tokens],
-                y[j][:].indirect(pos[:, first // GROUP : (first + count) // GROUP]),
-                gates[:, g, tokens],
-                MULT,
-            )
+        def positions(g, tokens):
+            return (pos1_sb, pos2_sb)[g][:, tokens.start // GROUP : tokens.stop // GROUP]
 
-        def fetch(j, first, blocks, at):
-            values = turn.tile([P, blocks * P], F32, name="fetched%d_%d" % (j, first), offset=at, align_bytes=64)
-            pos = pos1_sb[:, first * P // GROUP : (first + blocks) * P // GROUP]
-            nc.scalar.activation(values[:], y[j][:].indirect(pos), COPY)
-            into = bank(TURN_BANK[(j, first)], [P, BLOCKS, P], "turned")
-            for b in range(blocks):
-                turned[(j, first + b)] = into[:, b, :]
-                nc.tensor.transpose(into[:, b, :], values[:, b * P : (b + 1) * P], ident[:])
+        def pick(j, g, tokens):
+            nc.vector.tensor_tensor(picked[j][:, g, tokens], y[j][:].indirect(positions(g, tokens)), gates[:, g, tokens], MULT)
 
-        def weigh(j):
-            for b in range(SCALAR_BLOCKS[j]):
-                at = SCALED_AT + 4 * (T * (j - 1) + P * b)
-                scaled[(j, b)] = turn.tile([P, P], F32, name="scaled%d_%d" % (j, b), offset=at, align_bytes=64)
-                nc.scalar.activation(scaled[(j, b)][:], turned[(j, b)], COPY, scale=gate_cols[:, b : b + 1])
+        def place(j, g, at):
+            fetched[(j, g)] = turn.tile([P, T], F32, name="fetched%d_%d" % (j, g), offset=at, align_bytes=64)
 
-        def turn_back(j, first, count):
-            back[(j, first)] = bank(BACK_BANK[(j, first)], [P, T], "back")
-            for b in range(first // P, (first + count) // P):
-                nc.tensor.transpose(back[(j, first)][:, b * P : (b + 1) * P], scaled[(j, b)][:], ident[:])
+        def fetch(j, g, tokens):
+            nc.scalar.activation(fetched[(j, g)][:, tokens], y[j][:].indirect(positions(g, tokens)), COPY)
 
-        def finish(j, first, count):
-            tokens = slice(first, first + count)
-            if j not in results:
-                results[j] = ring.tile([P, T], F32, name="result")
-            weighted = back[(j, first)][:, tokens] if (j, first) in back else picked[j][:, 0, tokens]
-            nc.vector.tensor_tensor(results[j][:, tokens], weighted, picked[j][:, 1, tokens], ADD)
+        def weigh(j, g, tokens):
+            nc.vector.tensor_tensor(picked[j][:, g, tokens], fetched[(j, g)][:, tokens], gates[:, g, tokens], MULT)
+
+        def finish(j, tokens):
+            nc.vector.tensor_tensor(results[j][:, tokens], picked[j][:, 0, tokens], picked[j][:, 1, tokens], ADD)
             nc.sync.dma_start(out[j * P : (j + 1) * P, tokens], results[j][:, tokens])
 
         xg_first = keep.tile([P, C], U32, name="xg_first", align_bytes=64)
@@ -274,8 +243,6 @@ def tile_moe_pkd_mlp_silu_kernel(
         nc.sync.dma_start(pos1_sb[:], pos1)
         nc.sync.dma_start(pos2_sb[:], pos2)
         nc.sync.dma_start(gates[:], gate[:, 0:P, :].rearrange("g p t -> p g t"))
-        with nc.allow_non_contiguous_dma(reason="one weight a partition"):
-            nc.sync.dma_start(gate_cols[:], gate[0, 0, :].rearrange("(b p) -> p b", p=P))
 
         for e in range(1, E):
             base = RAW_BYTES * (e - 1)
@@ -320,29 +287,33 @@ def tile_moe_pkd_mlp_silu_kernel(
             for first in (0, 4):
                 evacuate(j, first, first + 4, nc.scalar.copy)
 
-        split = SCALAR_BLOCKS[2] * P
-        pick(0, 1, 0, T)
-        pick(0, 0, 0, T)
-        pick(1, 1, 0, T)
-        finish(0, 0, T)
-        pick(2, 1, 0, T)
-        pick(3, 1, 0, T)
-        fetch(1, 0, BLOCKS, CODES_AT + 4 * T)
-        fetch(2, 0, SCALAR_BLOCKS[2], CODES_AT)
-        fetch(3, 0, 2, LATE_AT)
-        weigh(1)
-        turn_back(1, 0, T)
-        pick(2, 0, split, T - split)
-        weigh(2)
-        turn_back(2, 0, split)
-        fetch(3, 2, 2, SCALED_AT)
-        finish(1, 0, T)
-        finish(2, split, T - split)
-        weigh(3)
-        turn_back(3, 0, 2 * P)
-        turn_back(3, 2 * P, P)
-        turn_back(3, 3 * P, P)
-        finish(2, 0, split)
-        finish(3, 0, 2 * P)
-        finish(3, 2 * P, P)
-        finish(3, 3 * P, P)
+        place(1, 0, CODES_AT + 4 * T)
+        place(2, 0, CODES_AT)
+        place(2, 1, CODES_AT + 8 * T)
+        place(3, 0, LATE_AT)
+        place(3, 1, LATE_AT + 4 * T)
+        every, head, tail = slice(0, T), slice(0, T // 2), slice(T // 2, T)
+        third, last = slice(T // 2, 3 * T // 4), slice(3 * T // 4, T)
+        pick(0, 1, every)
+        pick(0, 0, every)
+        pick(1, 1, every)
+        finish(0, every)
+        fetch(1, 0, every)
+        fetch(2, 0, every)
+        fetch(2, 1, every)
+        for tokens in (head, tail):
+            fetch(3, 0, tokens)
+            fetch(3, 1, tokens)
+        weigh(1, 0, every)
+        weigh(2, 0, every)
+        finish(1, every)
+        weigh(2, 1, every)
+        weigh(3, 0, head)
+        finish(2, every)
+        weigh(3, 1, head)
+        weigh(3, 0, tail)
+        finish(3, head)
+        weigh(3, 1, third)
+        weigh(3, 1, last)
+        finish(3, third)
+        finish(3, last)

@@ -1,6 +1,7 @@
 from contextlib import ExitStack
 
 import concourse.mybir as mybir
+from concourse.masks import make_identity
 
 K, T, E, C, H, N = 512, 512, 4, 256, 1024, 512
 SLOTS = E * C
@@ -14,12 +15,18 @@ GROUP = 16
 QUADRANT = 32
 ROWS = 4
 BANKS = 8
+BLOCKS = T // P
+
+SPLIT = 256
 
 RAW_BYTES = 2 * H
 CODES_AT = RAW_BYTES * (E - 1)
 LATE_AT = CODES_AT + 4 * (E - 1) * H_PASSES * C
+Y_AT = LATE_AT + 8 * T
+PICKED_AT = Y_AT + 4 * SLOTS
 
 SUM_BANK = {(0, 0): 0, (1, 0): 1, (2, 0): 2, (0, 4): 3, (1, 4): 4, (0, 7): 5, (2, 4): 6, (3, 0): 5, (3, 4): 4}
+GATE_BANK = (0, 1)
 
 F32 = mybir.dt.float32
 BF16 = mybir.dt.bfloat16
@@ -57,8 +64,11 @@ def tile_moe_pkd_mlp_silu_kernel(
             w2w[(pair, side)] = keep.tile([P, 2 * H_PASSES, N], U8, name="w2w%d%d" % (pair, side), align_bytes=64)
         w2_plane = keep.tile([P, E * H_PASSES, N], U8, name="w2_plane", align_bytes=64)
         gates = keep.tile([P, 2, T], F32, name="gates")
+        gate_cols = [keep.tile([P, BLOCKS], F32, name="gate_cols%d" % g) for g in range(2)]
+        ident = keep.tile([P, P], F32, name="ident")
         h_plane = keep.tile([P, E, H_PASSES, C], U8, name="h_plane", align_bytes=64)
-        y = [keep.tile([P, SLOTS], F32, name="y%d" % j) for j in range(N_TILES)]
+        y = {j: keep.tile([P, SLOTS], F32, name="y%d" % j) for j in (0, 2, 3)}
+        y[1] = turn.tile([P, SLOTS], F32, name="y1", offset=Y_AT, align_bytes=64)
 
         w1_raw = {0: keep.tile([P, RAW_BYTES], U8, name="w1_raw0", align_bytes=64)}
         w1s_raw = turn.tile([P, H], U8, name="w1s_raw", offset=0, align_bytes=64)
@@ -71,6 +81,7 @@ def tile_moe_pkd_mlp_silu_kernel(
         for e in range(1, E):
             nc.vector.memset(w1_plane[e][3 * QUADRANT : P, :].bitcast(I32), 0)
         nc.vector.memset(w2_plane[:].rearrange("p a n -> p (a n)").bitcast(I32), 0)
+        make_identity(nc, ident[:])
 
         def load_x_scales(queue, q):
             rows = x_scales[0, ROWS * q : ROWS * (q + 1), :].bitcast(I32)
@@ -192,9 +203,10 @@ def tile_moe_pkd_mlp_silu_kernel(
         def evacuate(j, first, last, copy):
             copy(out=y[j][:, first * CHUNK : last * CHUNK], in_=sums[(j, first)][:, 0 : (last - first) * CHUNK])
 
-        picked = [keep.tile([P, 2, T], F32, name="picked%d" % j) for j in range(N_TILES)]
-        results = [keep.tile([P, T], F32, name="result%d" % j) for j in range(N_TILES)]
-        fetched = {}
+        picked = {j: keep.tile([P, 2, T], F32, name="picked%d" % j) for j in (0, 2, 3)}
+        picked[1] = turn.tile([P, 2, T], F32, name="picked1", offset=PICKED_AT, align_bytes=64)
+        results = {j: keep.tile([P, T], F32, name="result%d" % j) for j in (1, 2, 3)}
+        fetched, spread = {}, []
 
         def positions(g, tokens):
             return (pos1_sb, pos2_sb)[g][:, tokens.start // GROUP : tokens.stop // GROUP]
@@ -209,10 +221,10 @@ def tile_moe_pkd_mlp_silu_kernel(
             nc.scalar.activation(fetched[(j, g)][:, tokens], y[j][:].indirect(positions(g, tokens)), COPY)
 
         def weigh(j, g, tokens):
-            nc.vector.tensor_tensor(picked[j][:, g, tokens], fetched[(j, g)][:, tokens], gates[:, g, tokens], MULT)
+            nc.vector.tensor_tensor(picked[j][:, g, tokens], fetched[(j, g)][:, tokens], spread[g][:, tokens], MULT)
 
-        def finish(j, tokens):
-            nc.vector.tensor_tensor(results[j][:, tokens], picked[j][:, 0, tokens], picked[j][:, 1, tokens], ADD)
+        def finish(j, tokens, engine=nc.vector):
+            engine.tensor_tensor(results[j][:, tokens], picked[j][:, 0, tokens], picked[j][:, 1, tokens], ADD)
             nc.sync.dma_start(out[j * P : (j + 1) * P, tokens], results[j][:, tokens])
 
         xg_first = keep.tile([P, C], U32, name="xg_first", align_bytes=64)
@@ -243,6 +255,9 @@ def tile_moe_pkd_mlp_silu_kernel(
         nc.sync.dma_start(pos1_sb[:], pos1)
         nc.sync.dma_start(pos2_sb[:], pos2)
         nc.sync.dma_start(gates[:], gate[:, 0:P, :].rearrange("g p t -> p g t"))
+        with nc.allow_non_contiguous_dma(reason="one weight a partition"):
+            for g in range(2):
+                nc.sync.dma_start(gate_cols[g][:], gate[g, 0, :].rearrange("(b p) -> p b", p=P))
 
         for e in range(1, E):
             base = RAW_BYTES * (e - 1)
@@ -294,26 +309,37 @@ def tile_moe_pkd_mlp_silu_kernel(
         place(3, 1, LATE_AT + 4 * T)
         every, head, tail = slice(0, T), slice(0, T // 2), slice(T // 2, T)
         third, last = slice(T // 2, 3 * T // 4), slice(3 * T // 4, T)
+        for g in range(2):
+            spread.append(bank(GATE_BANK[g], [P, T], "spread"))
+            for b in range(BLOCKS):
+                column = gate_cols[g][:, b : b + 1].to_broadcast([P, P])
+                nc.tensor.transpose(spread[g][:, b * P : (b + 1) * P], column, ident[:])
         pick(0, 1, every)
         pick(0, 0, every)
+        pick(2, 1, slice(SPLIT, T))
         pick(1, 1, every)
-        finish(0, every)
         fetch(1, 0, every)
         fetch(2, 0, every)
-        fetch(2, 1, every)
-        for tokens in (head, tail):
-            fetch(3, 0, tokens)
-            fetch(3, 1, tokens)
+        fetch(2, 1, slice(0, SPLIT))
+        fetch(3, 0, head)
+        fetch(3, 1, head)
+        fetch(3, 0, tail)
+        fetch(3, 1, third)
+        fetch(3, 1, last)
+        results[0] = turn.tile([P, T], F32, name="result0", offset=Y_AT, align_bytes=64)
+        finish(0, every, nc.gpsimd)
         weigh(1, 0, every)
         weigh(2, 0, every)
+        weigh(2, 1, slice(0, SPLIT))
         finish(1, every)
-        weigh(2, 1, every)
+        finish(2, tail)
+        results[2] = turn.tile([P, T // 2], F32, name="result2_head", offset=PICKED_AT, align_bytes=64)
+        finish(2, head, nc.gpsimd)
         weigh(3, 0, head)
-        finish(2, every)
         weigh(3, 1, head)
         weigh(3, 0, tail)
-        finish(3, head)
         weigh(3, 1, third)
+        finish(3, head)
         weigh(3, 1, last)
         finish(3, third)
         finish(3, last)

@@ -24,6 +24,7 @@ CODES_AT = RAW_BYTES * (E - 1)
 LATE_AT = CODES_AT + 4 * (E - 1) * H_PASSES * C
 Y_AT = LATE_AT + 8 * T
 PICKED_AT = Y_AT + 4 * SLOTS
+FIRST_AT = PICKED_AT + 8 * T
 
 SUM_BANK = {(0, 0): 0, (1, 0): 1, (2, 0): 2, (0, 4): 3, (1, 4): 4, (0, 7): 5, (2, 4): 6, (3, 0): 5, (3, 4): 4}
 GATE_BANK = (0, 1)
@@ -58,7 +59,7 @@ def tile_moe_pkd_mlp_silu_kernel(
         pos2_sb = keep.tile([P, T // GROUP], U16, name="pos2_sb")
         xw = keep.tile([P, T], I32, name="xw", align_bytes=64)
         xs = keep.tile([P, T], U8, name="xs", align_bytes=64)
-        w1_plane = [keep.tile([P, H], U8, name="w1_plane%d" % e, align_bytes=64) for e in range(E)]
+        w1_plane = [keep.tile([P, H], U8, name="w1_plane%d" % e, align_bytes=64) for e in range(2)]
         w2w = {(0, 0): turn.tile([P, 2 * H_PASSES, N], U8, name="w2w00", offset=LATE_AT, align_bytes=64)}
         for pair, side in ((0, 1), (1, 0), (1, 1)):
             w2w[(pair, side)] = keep.tile([P, 2 * H_PASSES, N], U8, name="w2w%d%d" % (pair, side), align_bytes=64)
@@ -70,18 +71,18 @@ def tile_moe_pkd_mlp_silu_kernel(
         y = {j: keep.tile([P, SLOTS], F32, name="y%d" % j) for j in (0, 2, 3)}
         y[1] = turn.tile([P, SLOTS], F32, name="y1", offset=Y_AT, align_bytes=64)
 
-        w1_raw = {0: keep.tile([P, RAW_BYTES], U8, name="w1_raw0", align_bytes=64)}
+        w1_raw = {0: turn.tile([P, RAW_BYTES], U8, name="w1_raw0", offset=FIRST_AT, align_bytes=64)}
         w1s_raw = turn.tile([P, H], U8, name="w1s_raw", offset=0, align_bytes=64)
         warm = keep.tile([P, 2], F32, name="warm")
         for e in range(1, E):
             w1_raw[e] = turn.tile([P, RAW_BYTES], U8, name="w1_raw%d" % e, offset=RAW_BYTES * e, align_bytes=64)
 
-        nc.gpsimd.memset(w1s_raw[:].bitcast(I32), 0)
+        nc.vector.memset(w1s_raw[:].bitcast(I32), 0)
         nc.vector.memset(warm[:, 0:1], 0.0)
-        for e in range(1, E):
-            nc.vector.memset(w1_plane[e][3 * QUADRANT : P, :].bitcast(I32), 0)
+        nc.vector.memset(ident[:], 0.0)
+        nc.vector.memset(w1_plane[1][3 * QUADRANT : P, :].bitcast(I32), 0)
         nc.vector.memset(w2_plane[:].rearrange("p a n -> p (a n)").bitcast(I32), 0)
-        make_identity(nc, ident[:])
+        make_identity(nc, ident[:], nomemset=True)
 
         def load_x_scales(queue, q):
             rows = x_scales[0, ROWS * q : ROWS * (q + 1), :].bitcast(I32)
@@ -241,6 +242,8 @@ def tile_moe_pkd_mlp_silu_kernel(
         first_layer(0, 1)
         first_layer(1, 1)
 
+        for e in range(2, E):
+            w1_plane.append(turn.tile([P, H], U8, name="w1_plane%d" % e, offset=FIRST_AT + H * (e - 2), align_bytes=64))
         for s in range(H_PASSES):
             move_plane(1, slice(s * K_PASS, (s + 1) * K_PASS))
         for e in range(2, E):

@@ -319,8 +319,8 @@ def tile_moe_pkd_mlp_silu_kernel(
                 nc.tensor.transpose(spread[g][:, b * P : (b + 1) * P], column, ident[:])
         pick(0, 1, every)
         pick(0, 0, every)
-        pick(2, 1, slice(SPLIT, T))
         pick(1, 1, every)
+        pick(2, 1, slice(SPLIT, T))
         fetch(1, 0, every)
         fetch(2, 0, every)
         fetch(2, 1, slice(0, SPLIT))

@@ -26,8 +26,8 @@ Y_AT = LATE_AT + 8 * T
 PICKED_AT = Y_AT + 4 * SLOTS
 FIRST_AT = PICKED_AT + 8 * T
 
-SUM_BANK = {(0, 0): 0, (1, 0): 1, (2, 0): 2, (0, 4): 3, (1, 4): 4, (0, 7): 5, (2, 4): 6, (3, 0): 5, (3, 4): 4}
-GATE_BANK = (0, 1)
+SUM_BANK = {(0, 0): 0, (1, 0): 1, (2, 0): 2, (0, 4): 3, (1, 4): 4, (0, 7): 5, (2, 4): 6, (3, 0): 0, (3, 4): 4, (1, 6): 7}
+GATE_BANK = (2, 1)
 
 F32 = mybir.dt.float32
 BF16 = mybir.dt.bfloat16
@@ -251,8 +251,8 @@ def tile_moe_pkd_mlp_silu_kernel(
         w2s_rows = w2_scales.rearrange("e s (q r) n -> r q (e s) n", r=ROWS)
         for r in range(ROWS):
             nc.sync.dma_start(w2_plane[r:P:QUADRANT, :, :].bitcast(I32), w2s_rows[r].bitcast(I32))
-        for side in range(2):
-            for pair in range(2):
+        for pair in range(2):
+            for side in range(2):
                 rows = w2_words[2 * pair : 2 * pair + 2, :, :, side * N : (side + 1) * N]
                 nc.sync.dma_start(w2w[(pair, side)][:].bitcast(I32), rows.rearrange("e s p b -> p (e s) b").bitcast(I32))
         nc.sync.dma_start(pos1_sb[:], pos1)
@@ -285,25 +285,30 @@ def tile_moe_pkd_mlp_silu_kernel(
             second_layer(j, 0, 0)
             second_layer(j, 2, 0)
             evacuate(j, 0, 4, nc.vector.tensor_copy)
+        second_layer(2, 0, 0)
+        second_layer(2, 2, 0)
         second_layer(0, 4, 4)
+        second_layer(3, 0, 0)
+        second_layer(3, 2, 0)
+        second_layer(1, 4, 4)
         late = turn.tile([P, H_PASSES, C], U32, name="late", offset=LATE_AT, align_bytes=64)
         h_codes.append(late[:])
         quantize(E - 1, 0, slice(0, C))
         quantize(E - 1, 1, slice(0, CHUNK))
+        second_layer(0, 6, 4, 1)
         quantize(E - 1, 1, slice(CHUNK, C))
         second_layer(0, 7, 7, 1)
-        second_layer(0, 6, 4, 1)
-        evacuate(0, 7, 8, nc.scalar.copy)
-        evacuate(0, 4, 7, nc.vector.tensor_copy)
-        second_layer(1, 4, 4)
-        second_layer(1, 6, 4)
-        evacuate(1, 4, 8, nc.scalar.copy)
         for j in range(2, N_TILES):
-            for first in (0, 4):
-                second_layer(j, first, first)
-                second_layer(j, first + 2, first)
-            for first in (0, 4):
-                evacuate(j, first, first + 4, nc.scalar.copy)
+            evacuate(j, 0, 4, nc.scalar.copy)
+        evacuate(1, 4, 6, nc.vector.tensor_copy)
+        evacuate(0, 4, 7, nc.vector.tensor_copy)
+        evacuate(0, 7, 8, nc.vector.tensor_copy)
+        second_layer(1, 6, 6)
+        evacuate(1, 6, 8, nc.scalar.copy)
+        for j in range(2, N_TILES):
+            second_layer(j, 4, 4)
+            second_layer(j, 6, 4)
+            evacuate(j, 4, 8, nc.scalar.copy)
 
         place(1, 0, CODES_AT + 4 * T)
         place(2, 0, CODES_AT)

@@ -215,8 +215,8 @@ def tile_moe_pkd_mlp_silu_kernel(
         def pick(j, g, tokens):
             nc.vector.tensor_tensor(picked[j][:, g, tokens], y[j][:].indirect(positions(g, tokens)), gates[:, g, tokens], MULT)
 
-        def place(j, g, at):
-            fetched[(j, g)] = turn.tile([P, T], F32, name="fetched%d_%d" % (j, g), offset=at, align_bytes=64)
+        def place(j, g, at, count=T):
+            fetched[(j, g)] = turn.tile([P, count], F32, name="fetched%d_%d" % (j, g), offset=at, align_bytes=64)
 
         def fetch(j, g, tokens):
             nc.scalar.activation(fetched[(j, g)][:, tokens], y[j][:].indirect(positions(g, tokens)), COPY)
@@ -311,8 +311,9 @@ def tile_moe_pkd_mlp_silu_kernel(
             evacuate(j, 4, 8, nc.scalar.copy)
 
         place(1, 0, CODES_AT + 4 * T)
+        place(1, 1, CODES_AT + 10 * T, P)
         place(2, 0, CODES_AT)
-        place(2, 1, CODES_AT + 8 * T)
+        place(2, 1, CODES_AT + 8 * T, SPLIT)
         place(3, 0, LATE_AT)
         place(3, 1, LATE_AT + 4 * T)
         every, head, tail = slice(0, T), slice(0, T // 2), slice(T // 2, T)
@@ -324,9 +325,10 @@ def tile_moe_pkd_mlp_silu_kernel(
                 nc.tensor.transpose(spread[g][:, b * P : (b + 1) * P], column, ident[:])
         pick(0, 1, every)
         pick(0, 0, every)
-        pick(1, 1, every)
+        pick(1, 1, slice(P, T))
         pick(2, 1, slice(SPLIT, T))
         fetch(1, 0, every)
+        fetch(1, 1, slice(0, P))
         fetch(2, 0, every)
         fetch(2, 1, slice(0, SPLIT))
         fetch(3, 0, head)
@@ -337,6 +339,7 @@ def tile_moe_pkd_mlp_silu_kernel(
         results[0] = turn.tile([P, T], F32, name="result0", offset=Y_AT, align_bytes=64)
         finish(0, every, nc.gpsimd)
         weigh(1, 0, every)
+        weigh(1, 1, slice(0, P))
         weigh(2, 0, every)
         weigh(2, 1, slice(0, SPLIT))
         finish(1, every)

from contextlib import ExitStack

import concourse.mybir as mybir
from concourse.masks import make_identity

K, T, E, C, H, N = 512, 512, 4, 256, 1024, 512
SLOTS = E * C
P = 128
PACK = 4
K_PASS = P * PACK
H_PASSES = H // K_PASS
N_TILES = N // P
CHUNK = 128
GROUP = 16
QUADRANT = 32
ROWS = 4
BANKS = 8
BLOCKS = T // P

SPLIT = 256

RAW_BYTES = 2 * H
CODES_AT = RAW_BYTES * (E - 1)
LATE_AT = CODES_AT + 4 * (E - 1) * H_PASSES * C
Y_AT = LATE_AT + 8 * T
PICKED_AT = Y_AT + 4 * SLOTS
FIRST_AT = PICKED_AT + 8 * T

SUM_BANK = {(0, 0): 0, (1, 0): 1, (2, 0): 2, (0, 4): 3, (1, 4): 4, (0, 7): 5, (2, 4): 6, (3, 0): 0, (3, 4): 4, (1, 6): 7}
GATE_BANK = (2, 1)

F32 = mybir.dt.float32
BF16 = mybir.dt.bfloat16
I32 = mybir.dt.int32
U32 = mybir.dt.uint32
U16 = mybir.dt.uint16
U8 = mybir.dt.uint8
FP8X4 = mybir.dt.float8_e4m3fn_x4
FP4X4 = mybir.dt.float4_e2m1fn_x4
SILU = mybir.ActivationFunctionType.Silu
COPY = mybir.ActivationFunctionType.Copy
MULT = mybir.AluOpType.mult
ADD = mybir.AluOpType.add

FLOPS = 2 * SLOTS * (K * H + H * N)


def tile_moe_pkd_mlp_silu_kernel(
    tc, x_words, x_scales, w1_words, w1_scales, w2_words, w2_scales, gate, offs, pos1, pos2, out
):
    nc = tc.nc
    with ExitStack() as ctx:
        keep = ctx.enter_context(tc.tile_pool(name="keep", bufs=1))
        turn = ctx.enter_context(tc.tile_pool(name="turn", bufs=1))
        psum = ctx.enter_context(tc.psum_pool(name="psum", bufs=1))

        offs_sb = keep.tile([P, SLOTS // GROUP], U16, name="offs_sb")
        pos1_sb = keep.tile([P, T // GROUP], U16, name="pos1_sb")
        pos2_sb = keep.tile([P, T // GROUP], U16, name="pos2_sb")
        xw = keep.tile([P, T], I32, name="xw", align_bytes=64)
        xs = keep.tile([P, T], U8, name="xs", align_bytes=64)
        w1_plane = [keep.tile([P, H], U8, name="w1_plane%d" % e, align_bytes=64) for e in range(2)]
        w2w = {(0, 0): turn.tile([P, 2 * H_PASSES, N], U8, name="w2w00", offset=LATE_AT, align_bytes=64)}
        for pair, side in ((0, 1), (1, 0), (1, 1)):
            w2w[(pair, side)] = keep.tile([P, 2 * H_PASSES, N], U8, name="w2w%d%d" % (pair, side), align_bytes=64)
        w2_plane = keep.tile([P, E * H_PASSES, N], U8, name="w2_plane", align_bytes=64)
        gates = keep.tile([P, 2, T], F32, name="gates")
        gate_cols = [keep.tile([P, BLOCKS], F32, name="gate_cols%d" % g) for g in range(2)]
        ident = keep.tile([P, P], F32, name="ident")
        h_plane = keep.tile([P, E, H_PASSES, C], U8, name="h_plane", align_bytes=64)
        y = {j: keep.tile([P, SLOTS], F32, name="y%d" % j) for j in (0, 2, 3)}
        y[1] = turn.tile([P, SLOTS], F32, name="y1", offset=Y_AT, align_bytes=64)

        w1_raw = {0: turn.tile([P, RAW_BYTES], U8, name="w1_raw0", offset=FIRST_AT, align_bytes=64)}
        w1s_raw = turn.tile([P, H], U8, name="w1s_raw", offset=0, align_bytes=64)
        warm = keep.tile([P, 2], F32, name="warm")
        for e in range(1, E):
            w1_raw[e] = turn.tile([P, RAW_BYTES], U8, name="w1_raw%d" % e, offset=RAW_BYTES * e, align_bytes=64)

        nc.vector.memset(w1s_raw[:].bitcast(I32), 0)
        nc.vector.memset(warm[:, 0:1], 0.0)
        nc.vector.memset(ident[:], 0.0)
        nc.vector.memset(w1_plane[1][3 * QUADRANT : P, :].bitcast(I32), 0)
        nc.vector.memset(w2_plane[:].rearrange("p a n -> p (a n)").bitcast(I32), 0)
        make_identity(nc, ident[:], nomemset=True)

        def load_x_scales(queue, q):
            rows = x_scales[0, ROWS * q : ROWS * (q + 1), :].bitcast(I32)
            queue.dma_start(
                xs[QUADRANT * q : QUADRANT * (q + 1), :].bitcast(I32),
                rows.unsqueeze(0).to_broadcast([QUADRANT // ROWS, ROWS, T // 4]),
            )

        def load_w1_scales(queue, q):
            queue.dma_start(
                w1s_raw[QUADRANT * q : QUADRANT * q + ROWS * E, :].bitcast(I32),
                w1_scales[:, 0, ROWS * q : ROWS * (q + 1), :].bitcast(I32),
            )

        nc.sync.dma_start(offs_sb[:], offs)
        for q in range(P // QUADRANT):
            load_x_scales(nc.sync if q % 2 else nc.scalar, q)
        nc.scalar.dma_start(w1_raw[0][:].bitcast(I32), w1_words[0, 0].bitcast(I32))
        nc.sync.dma_start(xw[:], x_words[0].rearrange("p t r -> p (t r)").bitcast(I32))
        for q in range(P // QUADRANT):
            load_w1_scales(nc.sync if q else nc.scalar, q)
        nc.scalar.activation(out=warm[:, 1:2], in_=warm[:, 0:1], func=SILU)
        for e in range(1, E):
            nc.sync.dma_start(w1_raw[e][:].bitcast(I32), w1_words[e, 0].bitcast(I32))

        xg, xsg, w1w = {}, {}, {}

        def entries(first, count):
            return offs_sb[:, first * CHUNK // GROUP : (first + count) * CHUNK // GROUP]

        def gather_words(first, count, words):
            nc.vector.tensor_copy(words, xw[:].bitcast(U32).indirect(entries(first, count)))
            for i in range(count):
                xg[first + i] = words[:, i * CHUNK : (i + 1) * CHUNK]

        def gather_scales(first, count, scales):
            nc.vector.tensor_copy(scales, xs[:].indirect(entries(first, count)))
            for i in range(count):
                xsg[first + i] = scales[:, i * CHUNK : (i + 1) * CHUNK]

        def reorder_words(e, s, copy):
            w1w[(e, s)] = keep.tile([P, 2 * K_PASS], U8, name="w1w%d_%d" % (e, s), align_bytes=64)
            raw = w1_raw[e][:, 2 * K_PASS * s : 2 * K_PASS * (s + 1)]
            copy(
                out=w1w[(e, s)][:].bitcast(U16).rearrange("p (t m) -> p t m", t=PACK),
                in_=raw.bitcast(U16).rearrange("p (m t) -> p t m", t=PACK),
            )

        def reorder_scales(s, first, count):
            cols = slice(s * K_PASS, (s + 1) * K_PASS)
            nc.vector.tensor_copy(
                out=w1_plane[0][:, cols].rearrange("p (t m) -> p t m", t=PACK)[:, first : first + count, :],
                in_=w1s_raw[:, cols].rearrange("p (m t) -> p t m", t=PACK)[:, first : first + count, :],
            )

        def move_plane(e, cols):
            for first, count in ((0, 2 * QUADRANT), (2 * QUADRANT, QUADRANT), (3 * QUADRANT, ROWS)):
                nc.sync.dma_start(
                    w1_plane[e][first : first + count, cols].bitcast(I32),
                    w1_plane[0][first + ROWS * e : first + ROWS * e + count, cols].bitcast(I32),
                )

        def bank(b, shape, name):
            return psum.tile(shape, F32, name=name, tag="bank%d" % b)

        h_bf = {}
        groups = []

        def first_layer(c, s):
            e = c * CHUNK // C
            if (e, s) not in h_bf:
                h_bf[(e, s)] = keep.tile([P, C, PACK], BF16, name="h_bf%d_%d" % (e, s), align_bytes=64)
            place = c * CHUNK - e * C
            a = bank(len(groups) % BANKS, [P, PACK, CHUNK], "a")
            groups.append(a)
            for t in range(PACK):
                col = s * K_PASS + t * P
                nc.tensor.matmul_mx(
                    out=a[:, t, :],
                    lhsT=w1w[(e, s)][:, 2 * t * P : 2 * (t + 1) * P].bitcast(FP4X4),
                    lhsT_scale=w1_plane[e][:, col : col + P],
                    rhs=xg[c].bitcast(FP8X4),
                    rhs_scale=xsg[c],
                    start=True,
                    stop=True,
                )
            nc.scalar.activation(
                out=h_bf[(e, s)][:, place : place + CHUNK, :], in_=a[:].rearrange("p t c -> p c t"), func=SILU
            )

        h_codes = []

        def quantize(e, s, places):
            nc.vector.quantize_mx(
                out=h_codes[e][:, s, places].bitcast(FP8X4),
                scales=h_plane[:, e, s, places],
                in_=h_bf[(e, s)][:, places, :].rearrange("p c t -> p (c t)"),
            )

        sums = {}

        def second_layer(j, c, first, count=2):
            e = c * CHUNK // C
            places = slice(c * CHUNK - e * C, (c + count) * CHUNK - e * C)
            if (j, first) not in sums:
                sums[(j, first)] = bank(SUM_BANK[(j, first)], [P, 4 * CHUNK], "sums")
            words = w2w[(e // 2, j // 2)]
            for s in range(H_PASSES):
                nc.tensor.matmul_mx(
                    out=sums[(j, first)][:, (c - first) * CHUNK : (c - first + count) * CHUNK],
                    lhsT=words[:, (e % 2) * H_PASSES + s, 2 * (j % 2) * P : 2 * (j % 2 + 1) * P].bitcast(FP4X4),
                    lhsT_scale=w2_plane[:, e * H_PASSES + s, j * P : (j + 1) * P],
                    rhs=h_codes[e][:, s, places].bitcast(FP8X4),
                    rhs_scale=h_plane[:, e, s, places],
                    start=(s == 0),
                    stop=(s == H_PASSES - 1),
                )

        def evacuate(j, first, last, copy):
            copy(out=y[j][:, first * CHUNK : last * CHUNK], in_=sums[(j, first)][:, 0 : (last - first) * CHUNK])

        picked = {j: keep.tile([P, 2, T], F32, name="picked%d" % j) for j in (0, 2, 3)}
        picked[1] = turn.tile([P, 2, T], F32, name="picked1", offset=PICKED_AT, align_bytes=64)
        results = {j: keep.tile([P, T], F32, name="result%d" % j) for j in (1, 2, 3)}
        fetched, spread = {}, []

        def positions(g, tokens):
            return (pos1_sb, pos2_sb)[g][:, tokens.start // GROUP : tokens.stop // GROUP]

        def pick(j, g, tokens):
            nc.vector.tensor_tensor(picked[j][:, g, tokens], y[j][:].indirect(positions(g, tokens)), gates[:, g, tokens], MULT)

        def place(j, g, at, count=T):
            fetched[(j, g)] = turn.tile([P, count], F32, name="fetched%d_%d" % (j, g), offset=at, align_bytes=64)

        def fetch(j, g, tokens):
            nc.scalar.activation(fetched[(j, g)][:, tokens], y[j][:].indirect(positions(g, tokens)), COPY)

        def weigh(j, g, tokens):
            nc.vector.tensor_tensor(picked[j][:, g, tokens], fetched[(j, g)][:, tokens], spread[g][:, tokens], MULT)

        def finish(j, tokens, engine=nc.vector):
            engine.tensor_tensor(results[j][:, tokens], picked[j][:, 0, tokens], picked[j][:, 1, tokens], ADD)
            nc.sync.dma_start(out[j * P : (j + 1) * P, tokens], results[j][:, tokens])

        xg_first = keep.tile([P, C], U32, name="xg_first", align_bytes=64)
        xsg_first = keep.tile([P, 3 * CHUNK], U8, name="xsg_first", align_bytes=64)
        gather_scales(0, 3, xsg_first[:])
        gather_words(0, 2, xg_first[:])
        for s in range(H_PASSES):
            reorder_words(0, s, nc.scalar.copy)
        reorder_scales(0, 0, PACK // 2)
        reorder_scales(0, PACK // 2, PACK // 2)
        first_layer(0, 0)
        reorder_scales(1, 0, PACK)
        first_layer(1, 0)
        first_layer(0, 1)
        first_layer(1, 1)

        for e in range(2, E):
            w1_plane.append(turn.tile([P, H], U8, name="w1_plane%d" % e, offset=FIRST_AT + H * (e - 2), align_bytes=64))
        for s in range(H_PASSES):
            move_plane(1, slice(s * K_PASS, (s + 1) * K_PASS))
        for e in range(2, E):
            move_plane(e, slice(0, H))
        w2s_rows = w2_scales.rearrange("e s (q r) n -> r q (e s) n", r=ROWS)
        for r in range(ROWS):
            nc.sync.dma_start(w2_plane[r:P:QUADRANT, :, :].bitcast(I32), w2s_rows[r].bitcast(I32))
        for pair in range(2):
            for side in range(2):
                rows = w2_words[2 * pair : 2 * pair + 2, :, :, side * N : (side + 1) * N]
                nc.sync.dma_start(w2w[(pair, side)][:].bitcast(I32), rows.rearrange("e s p b -> p (e s) b").bitcast(I32))
        nc.sync.dma_start(pos1_sb[:], pos1)
        nc.sync.dma_start(pos2_sb[:], pos2)
        nc.sync.dma_start(gates[:], gate[:, 0:P, :].rearrange("g p t -> p g t"))
        with nc.allow_non_contiguous_dma(reason="one weight a partition"):
            for g in range(2):
                nc.sync.dma_start(gate_cols[g][:], gate[g, 0, :].rearrange("(b p) -> p b", p=P))

        for e in range(1, E):
            base = RAW_BYTES * (e - 1)
            scales = turn.tile([P, C], U8, name="xsg%d" % e, offset=base, align_bytes=64)
            words = turn.tile([P, C], U32, name="xg%d" % e, offset=base + C, align_bytes=64)
            missing = [c for c in (2 * e, 2 * e + 1) if c not in xsg]
            reorder_words(e, 0, nc.vector.tensor_copy)
            gather_words(2 * e, 2, words[:])
            gather_scales(missing[0], len(missing), scales[:, 0 : len(missing) * CHUNK])
            first_layer(2 * e, 0)
            first_layer(2 * e + 1, 0)
            reorder_words(e, 1, nc.vector.tensor_copy)
            first_layer(2 * e, 1)
            first_layer(2 * e + 1, 1)

        early = turn.tile([P, E - 1, H_PASSES, C], U32, name="early", offset=CODES_AT, align_bytes=64)
        for e in range(E - 1):
            h_codes.append(early[:, e, :, :])
            for s in range(H_PASSES):
                quantize(e, s, slice(0, C))
        for j in range(2):
            second_layer(j, 0, 0)
            second_layer(j, 2, 0)
            evacuate(j, 0, 4, nc.vector.tensor_copy)
        second_layer(2, 0, 0)
        second_layer(2, 2, 0)
        second_layer(0, 4, 4)
        second_layer(3, 0, 0)
        second_layer(3, 2, 0)
        second_layer(1, 4, 4)
        late = turn.tile([P, H_PASSES, C], U32, name="late", offset=LATE_AT, align_bytes=64)
        h_codes.append(late[:])
        quantize(E - 1, 0, slice(0, C))
        quantize(E - 1, 1, slice(0, CHUNK))
        second_layer(0, 6, 4, 1)
        quantize(E - 1, 1, slice(CHUNK, C))
        second_layer(0, 7, 7, 1)
        for j in range(2, N_TILES):
            evacuate(j, 0, 4, nc.scalar.copy)
        evacuate(1, 4, 6, nc.vector.tensor_copy)
        evacuate(0, 4, 7, nc.vector.tensor_copy)
        evacuate(0, 7, 8, nc.vector.tensor_copy)
        second_layer(1, 6, 6)
        evacuate(1, 6, 8, nc.scalar.copy)
        for j in range(2, N_TILES):
            second_layer(j, 4, 4)
            second_layer(j, 6, 4)
            evacuate(j, 4, 8, nc.scalar.copy)

        place(1, 0, CODES_AT + 4 * T)
        place(1, 1, CODES_AT + 10 * T, P)
        place(2, 0, CODES_AT)
        place(2, 1, CODES_AT + 8 * T, SPLIT)
        place(3, 0, LATE_AT)
        place(3, 1, LATE_AT + 4 * T)
        every, head, tail = slice(0, T), slice(0, T // 2), slice(T // 2, T)
        third, last = slice(T // 2, 3 * T // 4), slice(3 * T // 4, T)
        for g in range(2):
            spread.append(bank(GATE_BANK[g], [P, T], "spread"))
            for b in range(BLOCKS):
                column = gate_cols[g][:, b : b + 1].to_broadcast([P, P])
                nc.tensor.transpose(spread[g][:, b * P : (b + 1) * P], column, ident[:])
        pick(0, 1, every)
        pick(0, 0, every)
        pick(1, 1, slice(P, T))
        pick(2, 1, slice(SPLIT, T))
        fetch(1, 0, every)
        fetch(1, 1, slice(0, P))
        fetch(2, 0, every)
        fetch(2, 1, slice(0, SPLIT))
        fetch(3, 0, head)
        fetch(3, 1, head)
        fetch(3, 0, tail)
        fetch(3, 1, third)
        fetch(3, 1, last)
        results[0] = turn.tile([P, T], F32, name="result0", offset=Y_AT, align_bytes=64)
        finish(0, every, nc.gpsimd)
        weigh(1, 0, every)
        weigh(1, 1, slice(0, P))
        weigh(2, 0, every)
        weigh(2, 1, slice(0, SPLIT))
        finish(1, every)
        finish(2, tail)
        results[2] = turn.tile([P, T // 2], F32, name="result2_head", offset=PICKED_AT, align_bytes=64)
        finish(2, head, nc.gpsimd)
        weigh(3, 0, head)
        weigh(3, 1, head)
        weigh(3, 0, tail)
        weigh(3, 1, third)
        finish(3, head)
        weigh(3, 1, last)
        finish(3, third)
        finish(3, last)
